import numpy as np
import ml_dtypes


def mxq(x, axis, fmt="e4m3"):
    dtype, down = {"e4m3": (ml_dtypes.float8_e4m3fn, 7), "e5m2": (ml_dtypes.float8_e5m2, 14)}[fmt]
    v = np.moveaxis(np.asarray(x, np.float32).astype(ml_dtypes.bfloat16).astype(np.float64), axis, -1)
    blocks = v.reshape(v.shape[:-1] + (-1, 32))
    amax = np.abs(blocks).max(-1, keepdims=True)
    byte = np.maximum(np.where(amax > 0, np.frexp(amax)[1] - 1 + 127, 0) - down, 1)
    scale = np.exp2(byte - 127.0)
    codes = (blocks / scale).astype(np.float32).astype(dtype).astype(np.float64)
    return np.moveaxis((codes * scale).reshape(v.shape), -1, axis)


WIDE = False


def mx_kscale(k):
    if not WIDE:
        return np.ones(k)
    levels = np.array([10, -10, 5, -5, 0])
    if k % 512:
        return np.exp2(np.random.permutation(np.resize(levels, k // 32))).repeat(32)
    a = np.empty((k // 512, 16))
    for p in range(k // 512):
        a[p, :8] = np.random.permutation(np.resize(levels, 8))
        for g in range(8):
            far = levels[np.abs(levels - a[p, g]) >= 10]
            a[p, g + 8] = far[np.random.randint(len(far))]
    return np.exp2(a.ravel()).repeat(32)


def f64(x):
    return np.asarray(x).astype(np.float64)


def striped(idx):
    return np.tile(idx.reshape(-1, 16).T, (8, 1)).astype(np.uint16)


def unstriped(offs):
    return offs[:16].T.reshape(-1).astype(np.int64)


def pack_weight(w):
    k, n = w.shape
    w = f64(np.asarray(w, np.float32).astype(ml_dtypes.bfloat16)).reshape(k // 32, 32, n)
    amax = np.abs(w).max(1)
    byte = np.clip(np.where(amax > 0, np.frexp(amax)[1] - 1 + 127 - 7, 1), 1, 254)
    scaled = (w * np.exp2(127.0 - byte)[:, None, :]).reshape(k, n).astype(np.float32)
    words = np.ascontiguousarray(scaled.reshape(k // 512, 128, 4, n).transpose(0, 1, 3, 2)).astype(ml_dtypes.float8_e4m3fn).view(np.uint8)
    return words, np.ascontiguousarray(byte.astype(np.uint8).reshape(k // 512, 16, n))


def unpack_weight(words, scales):
    g, p, n, _ = words.shape
    vals = np.ascontiguousarray(words).view(ml_dtypes.float8_e4m3fn).astype(np.float64) * np.repeat(np.exp2(scales.astype(np.float64) - 127.0), 8, axis=1)[..., None]
    return vals.transpose(0, 1, 3, 2).reshape(g * 512, n)


K, T, E, C, N = 512, 1024, 16, 256, 128
TOP = 4


def by_expert(wq, xq):
    return np.concatenate([wq[e].T @ xq[:, e * C:(e + 1) * C] for e in range(E)], axis=1)


def setup_inputs():
    n = np.random.standard_normal
    s = mx_kscale(K)[:, None]
    deal = np.repeat(np.arange(E), C).reshape(TOP, T)[:, np.random.permutation(T)]
    deal = np.take_along_axis(deal, np.argsort(np.random.rand(TOP, T), axis=0), axis=0)
    for _ in range(8):
        s_, t_ = np.random.permutation(T).reshape(2, -1); r = np.random.randint(TOP, size=T // 2); x, y = deal[r, s_].copy(), deal[r, t_].copy()
        ok = ~((deal[:, s_] == y).any(0) | (deal[:, t_] == x).any(0)); deal[r[ok], s_[ok]] = y[ok]; deal[r[ok], t_[ok]] = x[ok]
    order = np.lexsort((np.random.rand(TOP * T), deal.reshape(-1)))
    slot_token = order % T; pos = np.empty(TOP * T, np.int64); pos[order] = np.arange(TOP * T); pos = pos.reshape(TOP, T)
    g = np.random.uniform(0.5, 1.5, (TOP, T)); g = g / g.sum(0)
    packed = [pack_weight(m) for m in n((E, K, N)) / np.sqrt(K) / s[None]]
    w_slot = np.empty(E * C)
    for r in range(TOP): w_slot[pos[r]] = g[r]
    return {
        "xT": (n((K, T)) * s).astype(np.float32),
        "w_words": np.stack([m[0] for m in packed]),
        "w_scales": np.stack([m[1] for m in packed]),
        "gate": np.tile(w_slot, (K, 1)).astype(np.float32),
        "offs": striped(slot_token),
        "pos1": striped(pos[0]),
        "pos2": striped(pos[1]),
        "pos3": striped(pos[2]),
        "pos4": striped(pos[3]),
    }


def reference(xT, w_words, w_scales, gate, offs, pos1, pos2, pos3, pos4):
    idx = unstriped(offs)
    w = np.stack([unpack_weight(w_words[e], w_scales[e]) for e in range(E)])
    xq = mxq(f64(gate) * f64(xT)[:, idx], 0, "e4m3")
    y = by_expert(w, xq)
    return y[:, unstriped(pos1)] + y[:, unstriped(pos2)] + y[:, unstriped(pos3)] + y[:, unstriped(pos4)]

@@ -1,0 +1,127 @@
+from contextlib import ExitStack
+
+import concourse.mybir as mybir
+
+K, T, E, C, N = 512, 1024, 16, 256, 128
+SLOTS = E * C
+P = 128
+PACK = 4
+FLOPS = 2 * K * N * SLOTS
+BYTES = 4 * K * T + E * K * N + E * 16 * N + 4 * SLOTS + 2 * P * (SLOTS + 4 * T) // 16 + 4 * N * T
+
+F32 = mybir.dt.float32
+BF16 = mybir.dt.bfloat16
+I32 = mybir.dt.int32
+U32 = mybir.dt.uint32
+U16 = mybir.dt.uint16
+U8 = mybir.dt.uint8
+FP8X4 = mybir.dt.float8_e4m3fn_x4
+MULT = mybir.AluOpType.mult
+ADD = mybir.AluOpType.add
+
+CHUNKS = [512, 512, 512, 512, 512, 512, 512, 256, 128, 128]
+GATE_PIECES = [512, 512, 1024, 1024, 1024]
+HALF = 512
+
+
+def tile_moe_pre_lin_none_kernel(
+    tc, xT, w_words, w_scales, gate, offs, pos1, pos2, pos3, pos4, out
+):
+    nc = tc.nc
+    with ExitStack() as ctx:
+        keep = ctx.enter_context(tc.tile_pool(name="keep", bufs=1))
+        ring = ctx.enter_context(tc.tile_pool(name="ring", bufs=3))
+        psum = ctx.enter_context(tc.psum_pool(name="psum", bufs=4))
+
+        slot_list = keep.tile([P, SLOTS // 16], U16, name="slot_list")
+        pos_lists = [keep.tile([P, T // 16], U16, name=f"pos_list{r}") for r in range(4)]
+        x_rows = [keep.tile([P, T], F32, name=f"x_rows{j}") for j in range(PACK)]
+        gates = [keep.tile([P, n], F32, name=f"gate{i}") for i, n in enumerate(GATE_PIECES)]
+        gate_starts = [sum(GATE_PIECES[:i]) for i in range(len(GATE_PIECES))]
+        w_codes = keep.tile([P, E, N * PACK], U8, name="w_codes", align_bytes=64)
+        w_plane = keep.tile([P, E, N], U8, name="w_plane", align_bytes=64)
+        y = keep.tile([P, SLOTS], F32, name="y")
+
+        x_by_row = xT.rearrange("(p j) t -> j p t", j=PACK)
+        gate_rows = gate.rearrange("(p j) s -> j p s", j=PACK)[0]
+        words_hbm = w_words.rearrange("e a p n r -> p (e a) (n r)").bitcast(I32)
+        scales_hbm = w_scales.rearrange("e a q n -> q (e a) n").bitcast(I32)
+
+        def load_gate(i):
+            nc.sync.dma_start(gates[i][:], gate_rows[:, gate_starts[i] : gate_starts[i] + GATE_PIECES[i]])
+
+        nc.vector.memset(w_plane[:].bitcast(I32), 0)
+        nc.sync.dma_start(slot_list[:], offs)
+        load_gate(0)
+        for j in range(PACK):
+            nc.sync.dma_start(x_rows[j][:], x_by_row[j])
+        load_gate(1)
+        for quad in range(4):
+            nc.sync.dma_start(
+                w_plane[32 * quad : 32 * quad + 4, :, :].bitcast(I32), scales_hbm[4 * quad : 4 * quad + 4]
+            )
+        nc.sync.dma_start(w_codes[:, : E // 2, :].bitcast(I32), words_hbm[:, : E // 2, :])
+        load_gate(2)
+        nc.sync.dma_start(w_codes[:, E // 2 :, :].bitcast(I32), words_hbm[:, E // 2 :, :])
+        load_gate(3)
+        load_gate(4)
+        for tile, pos in zip(pos_lists, (pos1, pos2, pos3, pos4)):
+            nc.sync.dma_start(tile[:], pos)
+
+        def gather(start, n):
+            piece = max(i for i, s in enumerate(gate_starts) if s <= start)
+            g0 = start - gate_starts[piece]
+            prod = ring.tile([P, PACK, n], F32, name="prod")
+            for j in range(PACK):
+                nc.vector.tensor_tensor(
+                    prod[:, j, :],
+                    x_rows[j][:].indirect(slot_list[:, start // 16 : (start + n) // 16]),
+                    gates[piece][:, g0 : g0 + n],
+                    MULT,
+                )
+            grouped = ring.tile([P, n, PACK], BF16, name="grouped", align_bytes=64)
+            nc.scalar.copy(
+                out=grouped[:].rearrange("p (c i) j -> p c j i", i=4),
+                in_=prod[:].rearrange("p j (c i) -> p c j i", i=4),
+            )
+            return grouped
+
+        def multiply(start, n, grouped):
+            codes = ring.tile([P, n], U32, name="codes", align_bytes=64)
+            plane = ring.tile([P, n], U8, name="plane", align_bytes=64)
+            nc.vector.quantize_mx(
+                out=codes[:].bitcast(FP8X4), scales=plane[:], in_=grouped[:].rearrange("p c j -> p (c j)")
+            )
+            acc = psum.tile([P, 512], F32, name="acc")
+            width = min(n, C)
+            for c0 in range(0, n, width):
+                e = (start + c0) // C
+                nc.tensor.matmul_mx(
+                    out=acc[:, c0 : c0 + width],
+                    lhsT=w_codes[:, e, :].bitcast(FP8X4),
+                    lhsT_scale=w_plane[:, e, :],
+                    rhs=codes[:, c0 : c0 + width].bitcast(FP8X4),
+                    rhs_scale=plane[:, c0 : c0 + width],
+                    start=True,
+                    stop=True,
+                )
+            nc.scalar.copy(out=y[:, start : start + n], in_=acc[:, :n])
+
+        starts = [sum(CHUNKS[:i]) for i in range(len(CHUNKS))]
+        pending = None
+        for start, n in zip(starts, CHUNKS):
+            grouped = gather(start, n)
+            if pending is not None:
+                multiply(*pending)
+            pending = (start, n, grouped)
+        multiply(*pending)
+
+        for t0 in range(0, T, HALF):
+            picked = [keep.tile([P, HALF], F32, name=f"picked{t0}_{r}") for r in range(4)]
+            sums = [keep.tile([P, HALF], F32, name=f"sum{t0}_{r}") for r in range(3)]
+            for r in range(4):
+                nc.vector.tensor_copy(picked[r][:], y[:].indirect(pos_lists[r][:, t0 // 16 : (t0 + HALF) // 16]))
+            nc.vector.tensor_tensor(sums[0][:], picked[0][:], picked[1][:], ADD)
+            nc.vector.tensor_tensor(sums[1][:], sums[0][:], picked[2][:], ADD)
+            nc.vector.tensor_tensor(sums[2][:], sums[1][:], picked[3][:], ADD)
+            nc.sync.dma_start(out[:, t0 : t0 + HALF], sums[2][:])

@@ -19,8 +19,11 @@ FP8X4 = mybir.dt.float8_e4m3fn_x4
 MULT = mybir.AluOpType.mult
 ADD = mybir.AluOpType.add
 
-CHUNKS = [512, 512, 512, 512, 512, 512, 512, 256, 128, 128]
-GATE_PIECES = [512, 512, 1024, 1024, 1024]
+CHUNKS = [512,1024,1024,512,512,256,128,128]
+GATE_PIECES = [512,1024,1024,1536]
+PAD = 32
+LAG = [1,1,2,1,1,2,2,2]
+VECTOR_EMPTIES = [7]
 HALF = 512
 
 
@@ -30,12 +33,11 @@ def tile_moe_pre_lin_none_kernel(
     nc = tc.nc
     with ExitStack() as ctx:
         keep = ctx.enter_context(tc.tile_pool(name="keep", bufs=1))
-        ring = ctx.enter_context(tc.tile_pool(name="ring", bufs=3))
-        psum = ctx.enter_context(tc.psum_pool(name="psum", bufs=4))
+        psum = ctx.enter_context(tc.psum_pool(name="psum", bufs=8))
 
         slot_list = keep.tile([P, SLOTS // 16], U16, name="slot_list")
         pos_lists = [keep.tile([P, T // 16], U16, name=f"pos_list{r}") for r in range(4)]
-        x_rows = [keep.tile([P, T], F32, name=f"x_rows{j}") for j in range(PACK)]
+        x_rows = [keep.tile([P, T + PAD], F32, name=f"x_rows{j}") for j in range(PACK)]
         gates = [keep.tile([P, n], F32, name=f"gate{i}") for i, n in enumerate(GATE_PIECES)]
         gate_starts = [sum(GATE_PIECES[:i]) for i in range(len(GATE_PIECES))]
         w_codes = keep.tile([P, E, N * PACK], U8, name="w_codes", align_bytes=64)
@@ -50,11 +52,16 @@ def tile_moe_pre_lin_none_kernel(
         def load_gate(i):
             nc.sync.dma_start(gates[i][:], gate_rows[:, gate_starts[i] : gate_starts[i] + GATE_PIECES[i]])
 
+        def load_x(j):
+            nc.sync.dma_start(x_rows[j][:, :T], x_by_row[j])
+
+        for j in range(PACK):
+            nc.vector.memset(x_rows[j][:, T:], 0.0)
         nc.vector.memset(w_plane[:].bitcast(I32), 0)
         nc.sync.dma_start(slot_list[:], offs)
         load_gate(0)
         for j in range(PACK):
-            nc.sync.dma_start(x_rows[j][:], x_by_row[j])
+            load_x(j)
         load_gate(1)
         for quad in range(4):
             nc.sync.dma_start(
@@ -64,64 +71,82 @@ def tile_moe_pre_lin_none_kernel(
         load_gate(2)
         nc.sync.dma_start(w_codes[:, E // 2 :, :].bitcast(I32), words_hbm[:, E // 2 :, :])
         load_gate(3)
-        load_gate(4)
         for tile, pos in zip(pos_lists, (pos1, pos2, pos3, pos4)):
             nc.sync.dma_start(tile[:], pos)
 
+        def gate_view(s0, s1):
+            piece = max(i for i, s in enumerate(gate_starts) if s <= s0)
+            assert s1 <= gate_starts[piece] + GATE_PIECES[piece]
+            return gates[piece], s0 - gate_starts[piece]
+
         def gather(start, n):
-            piece = max(i for i, s in enumerate(gate_starts) if s <= start)
-            g0 = start - gate_starts[piece]
-            prod = ring.tile([P, PACK, n], F32, name="prod")
+            prod = keep.tile([P, PACK, n], F32, name=f"prod{start}")
             for j in range(PACK):
-                nc.vector.tensor_tensor(
-                    prod[:, j, :],
-                    x_rows[j][:].indirect(slot_list[:, start // 16 : (start + n) // 16]),
-                    gates[piece][:, g0 : g0 + n],
-                    MULT,
-                )
-            grouped = ring.tile([P, n, PACK], BF16, name="grouped", align_bytes=64)
+                cuts = [s for s in gate_starts if start < s < start + n] if True else []
+                for s0, s1 in zip([start] + cuts, cuts + [start + n]):
+                    gate_tile, g0 = gate_view(s0, s1)
+                    nc.vector.tensor_tensor(
+                        prod[:, j, s0 - start : s1 - start],
+                        x_rows[j][:].indirect(slot_list[:, s0 // 16 : s1 // 16]),
+                        gate_tile[:, g0 : g0 + s1 - s0],
+                        MULT,
+                    )
+            grouped = keep.tile([P, n, PACK], BF16, name=f"grouped{start}", align_bytes=64)
             nc.scalar.copy(
                 out=grouped[:].rearrange("p (c i) j -> p c j i", i=4),
                 in_=prod[:].rearrange("p j (c i) -> p c j i", i=4),
             )
             return grouped
 
-        def multiply(start, n, grouped):
-            codes = ring.tile([P, n], U32, name="codes", align_bytes=64)
-            plane = ring.tile([P, n], U8, name="plane", align_bytes=64)
+        def multiply(index, start, n, grouped):
+            codes = keep.tile([P, n], U32, name=f"codes{start}", align_bytes=64)
+            plane = keep.tile([P, n], U8, name=f"plane{start}", align_bytes=64)
             nc.vector.quantize_mx(
                 out=codes[:].bitcast(FP8X4), scales=plane[:], in_=grouped[:].rearrange("p c j -> p (c j)")
             )
-            acc = psum.tile([P, 512], F32, name="acc")
             width = min(n, C)
-            for c0 in range(0, n, width):
-                e = (start + c0) // C
-                nc.tensor.matmul_mx(
-                    out=acc[:, c0 : c0 + width],
-                    lhsT=w_codes[:, e, :].bitcast(FP8X4),
-                    lhsT_scale=w_plane[:, e, :],
-                    rhs=codes[:, c0 : c0 + width].bitcast(FP8X4),
-                    rhs_scale=plane[:, c0 : c0 + width],
-                    start=True,
-                    stop=True,
-                )
-            nc.scalar.copy(out=y[:, start : start + n], in_=acc[:, :n])
+            for b0 in range(0, n, 512):
+                cols = min(512, n)
+                acc = psum.tile([P, 512], F32, name="acc")
+                for c0 in range(b0, b0 + cols, width):
+                    e = (start + c0) // C
+                    nc.tensor.matmul_mx(
+                        out=acc[:, c0 - b0 : c0 - b0 + width],
+                        lhsT=w_codes[:, e, :].bitcast(FP8X4),
+                        lhsT_scale=w_plane[:, e, :],
+                        rhs=codes[:, c0 : c0 + width].bitcast(FP8X4),
+                        rhs_scale=plane[:, c0 : c0 + width],
+                        start=True,
+                        stop=True,
+                    )
+                if index in VECTOR_EMPTIES:
+                    nc.vector.tensor_copy(out=y[:, start + b0 : start + b0 + cols], in_=acc[:, :cols])
+                else:
+                    nc.scalar.copy(out=y[:, start + b0 : start + b0 + cols], in_=acc[:, :cols])
 
         starts = [sum(CHUNKS[:i]) for i in range(len(CHUNKS))]
-        pending = None
-        for start, n in zip(starts, CHUNKS):
-            grouped = gather(start, n)
-            if pending is not None:
-                multiply(*pending)
-            pending = (start, n, grouped)
-        multiply(*pending)
+        groups = []
+        done = 0
+        for i, (start, n) in enumerate(zip(starts, CHUNKS)):
+            groups.append(gather(start, n))
+            while done <= i - LAG[done]:
+                multiply(done, starts[done], CHUNKS[done], groups[done])
+                done += 1
+        for i in range(done, len(CHUNKS)):
+            multiply(i, starts[i], CHUNKS[i], groups[i])
 
         for t0 in range(0, T, HALF):
             picked = [keep.tile([P, HALF], F32, name=f"picked{t0}_{r}") for r in range(4)]
             sums = [keep.tile([P, HALF], F32, name=f"sum{t0}_{r}") for r in range(3)]
             for r in range(4):
                 nc.vector.tensor_copy(picked[r][:], y[:].indirect(pos_lists[r][:, t0 // 16 : (t0 + HALF) // 16]))
-            nc.vector.tensor_tensor(sums[0][:], picked[0][:], picked[1][:], ADD)
-            nc.vector.tensor_tensor(sums[1][:], sums[0][:], picked[2][:], ADD)
-            nc.vector.tensor_tensor(sums[2][:], sums[1][:], picked[3][:], ADD)
-            nc.sync.dma_start(out[:, t0 : t0 + HALF], sums[2][:])
+            nc.gpsimd.tensor_tensor(sums[0][:], picked[0][:], picked[1][:], ADD)
+            nc.gpsimd.tensor_tensor(sums[1][:], sums[0][:], picked[2][:], ADD)
+            if t0 == 0:
+                nc.gpsimd.tensor_tensor(sums[2][:], sums[1][:], picked[3][:], ADD)
+                nc.sync.dma_start(out[:, t0 : t0 + HALF], sums[2][:])
+            else:
+                for h0, queue in ((0, nc.sync), (HALF // 2, nc.scalar)):
+                    cols = slice(h0, h0 + HALF // 2)
+                    nc.vector.tensor_tensor(sums[2][:, cols], sums[1][:, cols], picked[3][:, cols], ADD)
+                    queue.dma_start(out[:, t0 + h0 : t0 + h0 + HALF // 2], sums[2][:, cols])

@@ -19,12 +19,12 @@ FP8X4 = mybir.dt.float8_e4m3fn_x4
 MULT = mybir.AluOpType.mult
 ADD = mybir.AluOpType.add
 
-CHUNKS = [512,1024,1024,512,512,256,128,128]
-GATE_PIECES = [512,1024,1024,1536]
-PAD = 32
-LAG = [1,1,2,1,1,2,2,2]
-VECTOR_EMPTIES = [7]
+STEPS = [[0,1152],[1280,1024],[0,1024,"ss"],[1024,128,"s"],[2304,1024],[1280,1024,"ss"],[3328,512],[2304,1024,"ss"],[3840,256],[1152,128],[3328,512,"ss"],[3840,256,"s"],[1152,128,"v"]]
+GATE_PIECES = [128,384,768,1024,1792]
+PAD = 160
 HALF = 512
+SPLIT = 320
+BACK_ORDER = [(0, 0), (0, 1), (0, 2), (1, 0), (1, 1), (0, 3), (1, 2), (1, 3)]
 
 
 def tile_moe_pre_lin_none_kernel(
@@ -33,12 +33,13 @@ def tile_moe_pre_lin_none_kernel(
     nc = tc.nc
     with ExitStack() as ctx:
         keep = ctx.enter_context(tc.tile_pool(name="keep", bufs=1))
+        ring = ctx.enter_context(tc.tile_pool(name="ring", bufs=2))
         psum = ctx.enter_context(tc.psum_pool(name="psum", bufs=8))
 
         slot_list = keep.tile([P, SLOTS // 16], U16, name="slot_list")
         pos_lists = [keep.tile([P, T // 16], U16, name=f"pos_list{r}") for r in range(4)]
         x_rows = [keep.tile([P, T + PAD], F32, name=f"x_rows{j}") for j in range(PACK)]
-        gates = [keep.tile([P, n], F32, name=f"gate{i}") for i, n in enumerate(GATE_PIECES)]
+        gate_all = keep.tile([P, SLOTS], F32, name="gate_all")
         gate_starts = [sum(GATE_PIECES[:i]) for i in range(len(GATE_PIECES))]
         w_codes = keep.tile([P, E, N * PACK], U8, name="w_codes", align_bytes=64)
         w_plane = keep.tile([P, E, N], U8, name="w_plane", align_bytes=64)
@@ -49,46 +50,41 @@ def tile_moe_pre_lin_none_kernel(
         words_hbm = w_words.rearrange("e a p n r -> p (e a) (n r)").bitcast(I32)
         scales_hbm = w_scales.rearrange("e a q n -> q (e a) n").bitcast(I32)
 
-        def load_gate(i):
-            nc.sync.dma_start(gates[i][:], gate_rows[:, gate_starts[i] : gate_starts[i] + GATE_PIECES[i]])
+        def load_gate(i, queue=nc.sync):
+            cols = slice(gate_starts[i], gate_starts[i] + GATE_PIECES[i])
+            queue.dma_start(gate_all[:, cols], gate_rows[:, cols])
 
         def load_x(j):
             nc.sync.dma_start(x_rows[j][:, :T], x_by_row[j])
 
-        for j in range(PACK):
-            nc.vector.memset(x_rows[j][:, T:], 0.0)
         nc.vector.memset(w_plane[:].bitcast(I32), 0)
         nc.sync.dma_start(slot_list[:], offs)
         load_gate(0)
-        for j in range(PACK):
-            load_x(j)
+        load_x(0)
         load_gate(1)
+        load_gate(2)
+        for j in range(1, PACK):
+            load_x(j)
+        load_gate(3)
         for quad in range(4):
             nc.sync.dma_start(
                 w_plane[32 * quad : 32 * quad + 4, :, :].bitcast(I32), scales_hbm[4 * quad : 4 * quad + 4]
             )
         nc.sync.dma_start(w_codes[:, : E // 2, :].bitcast(I32), words_hbm[:, : E // 2, :])
-        load_gate(2)
         nc.sync.dma_start(w_codes[:, E // 2 :, :].bitcast(I32), words_hbm[:, E // 2 :, :])
-        load_gate(3)
+        load_gate(4)
         for tile, pos in zip(pos_lists, (pos1, pos2, pos3, pos4)):
             nc.sync.dma_start(tile[:], pos)
 
-        def gate_view(s0, s1):
-            piece = max(i for i, s in enumerate(gate_starts) if s <= s0)
-            assert s1 <= gate_starts[piece] + GATE_PIECES[piece]
-            return gates[piece], s0 - gate_starts[piece]
-
         def gather(start, n):
-            prod = keep.tile([P, PACK, n], F32, name=f"prod{start}")
+            prod = ring.tile([P, PACK, n], F32, name="prod")
             for j in range(PACK):
-                cuts = [s for s in gate_starts if start < s < start + n] if True else []
+                cuts = [s for s in gate_starts if start < s < start + n] if j == 0 else []
                 for s0, s1 in zip([start] + cuts, cuts + [start + n]):
-                    gate_tile, g0 = gate_view(s0, s1)
                     nc.vector.tensor_tensor(
                         prod[:, j, s0 - start : s1 - start],
                         x_rows[j][:].indirect(slot_list[:, s0 // 16 : s1 // 16]),
-                        gate_tile[:, g0 : g0 + s1 - s0],
+                        gate_all[:, s0:s1],
                         MULT,
                     )
             grouped = keep.tile([P, n, PACK], BF16, name=f"grouped{start}", align_bytes=64)
@@ -98,55 +94,68 @@ def tile_moe_pre_lin_none_kernel(
             )
             return grouped
 
-        def multiply(index, start, n, grouped):
+        def multiply(start, n, engines):
+            chunk = max(s for s in groups if s <= start)
             codes = keep.tile([P, n], U32, name=f"codes{start}", align_bytes=64)
             plane = keep.tile([P, n], U8, name=f"plane{start}", align_bytes=64)
             nc.vector.quantize_mx(
-                out=codes[:].bitcast(FP8X4), scales=plane[:], in_=grouped[:].rearrange("p c j -> p (c j)")
+                out=codes[:].bitcast(FP8X4),
+                scales=plane[:],
+                in_=groups[chunk][:, start - chunk : start - chunk + n, :].rearrange("p c j -> p (c j)"),
             )
             width = min(n, C)
-            for b0 in range(0, n, 512):
-                cols = min(512, n)
+            cols = n // len(engines)
+            for b, engine in enumerate(engines):
+                b0 = b * cols
                 acc = psum.tile([P, 512], F32, name="acc")
-                for c0 in range(b0, b0 + cols, width):
+                for c0 in range(b0, b0 + cols, min(width, cols)):
                     e = (start + c0) // C
+                    w = min(width, cols)
                     nc.tensor.matmul_mx(
-                        out=acc[:, c0 - b0 : c0 - b0 + width],
+                        out=acc[:, c0 - b0 : c0 - b0 + w],
                         lhsT=w_codes[:, e, :].bitcast(FP8X4),
                         lhsT_scale=w_plane[:, e, :],
-                        rhs=codes[:, c0 : c0 + width].bitcast(FP8X4),
-                        rhs_scale=plane[:, c0 : c0 + width],
+                        rhs=codes[:, c0 : c0 + w].bitcast(FP8X4),
+                        rhs_scale=plane[:, c0 : c0 + w],
                         start=True,
                         stop=True,
                     )
-                if index in VECTOR_EMPTIES:
+                if engine == "v":
                     nc.vector.tensor_copy(out=y[:, start + b0 : start + b0 + cols], in_=acc[:, :cols])
                 else:
                     nc.scalar.copy(out=y[:, start + b0 : start + b0 + cols], in_=acc[:, :cols])
 
-        starts = [sum(CHUNKS[:i]) for i in range(len(CHUNKS))]
-        groups = []
-        done = 0
-        for i, (start, n) in enumerate(zip(starts, CHUNKS)):
-            groups.append(gather(start, n))
-            while done <= i - LAG[done]:
-                multiply(done, starts[done], CHUNKS[done], groups[done])
-                done += 1
-        for i in range(done, len(CHUNKS)):
-            multiply(i, starts[i], CHUNKS[i], groups[i])
-
-        for t0 in range(0, T, HALF):
-            picked = [keep.tile([P, HALF], F32, name=f"picked{t0}_{r}") for r in range(4)]
-            sums = [keep.tile([P, HALF], F32, name=f"sum{t0}_{r}") for r in range(3)]
-            for r in range(4):
-                nc.vector.tensor_copy(picked[r][:], y[:].indirect(pos_lists[r][:, t0 // 16 : (t0 + HALF) // 16]))
-            nc.gpsimd.tensor_tensor(sums[0][:], picked[0][:], picked[1][:], ADD)
-            nc.gpsimd.tensor_tensor(sums[1][:], sums[0][:], picked[2][:], ADD)
-            if t0 == 0:
-                nc.gpsimd.tensor_tensor(sums[2][:], sums[1][:], picked[3][:], ADD)
-                nc.sync.dma_start(out[:, t0 : t0 + HALF], sums[2][:])
+        groups = {}
+        for step in STEPS:
+            if len(step) == 2:
+                groups[step[0]] = gather(*step)
             else:
-                for h0, queue in ((0, nc.sync), (HALF // 2, nc.scalar)):
-                    cols = slice(h0, h0 + HALF // 2)
-                    nc.vector.tensor_tensor(sums[2][:, cols], sums[1][:, cols], picked[3][:, cols], ADD)
-                    queue.dma_start(out[:, t0 + h0 : t0 + h0 + HALF // 2], sums[2][:, cols])
+                multiply(*step)
+
+        def fetch(half, r):
+            picked = keep.tile([P, HALF], F32, name=f"picked{half}_{r}")
+            cols = slice(half * HALF // 16, (half + 1) * HALF // 16)
+            nc.vector.tensor_copy(picked[:], y[:].indirect(pos_lists[r][:, cols]))
+            return picked
+
+        sums = {}
+        for half, r in BACK_ORDER[:-2]:
+            picked = fetch(half, r)
+            if r == 0:
+                sums[half] = picked
+                continue
+            total = keep.tile([P, HALF], F32, name=f"sum{half}_{r}")
+            nc.gpsimd.tensor_tensor(total[:], sums[half][:], picked[:], ADD)
+            sums[half] = total
+        nc.sync.dma_start(out[:, :HALF], sums[0][:])
+
+        left, right = slice(0, SPLIT), slice(SPLIT, HALF)
+        third = fetch(1, 2)
+        three = keep.tile([P, HALF], F32, name="three")
+        nc.gpsimd.tensor_tensor(three[:, left], sums[1][:, left], third[:, left], ADD)
+        fourth = fetch(1, 3)
+        four = keep.tile([P, HALF], F32, name="four")
+        nc.vector.tensor_tensor(three[:, right], sums[1][:, right], third[:, right], ADD)
+        for part, queue in ((left, nc.sync), (right, nc.scalar)):
+            nc.vector.tensor_tensor(four[:, part], three[:, part], fourth[:, part], ADD)
+            queue.dma_start(out[:, HALF + part.start : HALF + part.stop], four[:, part])

@@ -19,9 +19,9 @@ FP8X4 = mybir.dt.float8_e4m3fn_x4
 MULT = mybir.AluOpType.mult
 ADD = mybir.AluOpType.add
 
-STEPS = [[0,1152],[1280,1024],[0,1024,"ss"],[1024,128,"s"],[2304,1024],[1280,1024,"ss"],[3328,512],[2304,1024,"ss"],[3840,256],[1152,128],[3328,512,"ss"],[3840,256,"s"],[1152,128,"v"]]
-GATE_PIECES = [128,384,768,1024,1792]
-PAD = 160
+STEPS = [[0,1408],[1536,1024],[0,1024,"ss"],[1024,256,"s"],[1280,128,"s"],[2560,768],[1536,1024,"ss"],[3328,512],[2560,512,"s"],[3072,256,"s"],[3840,256],[1408,128],[3328,512,"ss"],[3840,256,"s"],[1408,128,"v"]]
+GATE_PIECES = [160,480,896,1024,1536]
+PAD = 416
 HALF = 512
 SPLIT = 320
 BACK_ORDER = [(0, 0), (0, 1), (0, 2), (1, 0), (1, 1), (0, 3), (1, 2), (1, 3)]
@@ -58,9 +58,9 @@ def tile_moe_pre_lin_none_kernel(
             nc.sync.dma_start(x_rows[j][:, :T], x_by_row[j])
 
         nc.vector.memset(w_plane[:].bitcast(I32), 0)
+        load_x(0)
         nc.sync.dma_start(slot_list[:], offs)
         load_gate(0)
-        load_x(0)
         load_gate(1)
         load_gate(2)
         for j in range(1, PACK):

@@ -24,7 +24,6 @@ GATE_PIECES = [160,480,896,1024,1536]
 PAD = 416
 HALF = 512
 SPLIT = 320
-BACK_ORDER = [(0, 0), (0, 1), (0, 2), (1, 0), (1, 1), (0, 3), (1, 2), (1, 3)]
 
 
 def tile_moe_pre_lin_none_kernel(
@@ -132,30 +131,17 @@ def tile_moe_pre_lin_none_kernel(
             else:
                 multiply(*step)
 
-        def fetch(half, r):
-            picked = keep.tile([P, HALF], F32, name=f"picked{half}_{r}")
-            cols = slice(half * HALF // 16, (half + 1) * HALF // 16)
-            nc.vector.tensor_copy(picked[:], y[:].indirect(pos_lists[r][:, cols]))
-            return picked
+        def picked(r, cols):
+            return y[:].indirect(pos_lists[r][:, cols.start // 16 : cols.stop // 16])
 
-        sums = {}
-        for half, r in BACK_ORDER[:-2]:
-            picked = fetch(half, r)
-            if r == 0:
-                sums[half] = picked
-                continue
-            total = keep.tile([P, HALF], F32, name=f"sum{half}_{r}")
-            nc.gpsimd.tensor_tensor(total[:], sums[half][:], picked[:], ADD)
-            sums[half] = total
-        nc.sync.dma_start(out[:, :HALF], sums[0][:])
-
-        left, right = slice(0, SPLIT), slice(SPLIT, HALF)
-        third = fetch(1, 2)
-        three = keep.tile([P, HALF], F32, name="three")
-        nc.gpsimd.tensor_tensor(three[:, left], sums[1][:, left], third[:, left], ADD)
-        fourth = fetch(1, 3)
-        four = keep.tile([P, HALF], F32, name="four")
-        nc.vector.tensor_tensor(three[:, right], sums[1][:, right], third[:, right], ADD)
-        for part, queue in ((left, nc.sync), (right, nc.scalar)):
-            nc.vector.tensor_tensor(four[:, part], three[:, part], fourth[:, part], ADD)
-            queue.dma_start(out[:, HALF + part.start : HALF + part.stop], four[:, part])
+        sums = [keep.tile([P, T], F32, name=f"sum{r}") for r in range(4)]
+        halves = [slice(0, HALF), slice(HALF, T)]
+        for cols in halves:
+            nc.vector.tensor_copy(sums[0][:, cols], picked(0, cols))
+        for r in (1, 2):
+            for cols in halves:
+                nc.vector.tensor_tensor(sums[r][:, cols], picked(r, cols), sums[r - 1][:, cols], ADD)
+        last = [slice(0, HALF), slice(HALF, HALF + SPLIT), slice(HALF + SPLIT, T)]
+        for cols, queue in zip(last, (nc.sync, nc.scalar, nc.sync)):
+            nc.vector.tensor_tensor(sums[3][:, cols], picked(3, cols), sums[2][:, cols], ADD)
+            queue.dma_start(out[:, cols], sums[3][:, cols])

@@ -6,6 +6,7 @@ K, T, E, C, N = 512, 1024, 16, 256, 128
 SLOTS = E * C
 P = 128
 PACK = 4
+BANK = 512
 FLOPS = 2 * K * N * SLOTS
 BYTES = 4 * K * T + E * K * N + E * 16 * N + 4 * SLOTS + 2 * P * (SLOTS + 4 * T) // 16 + 4 * N * T
 
@@ -19,11 +20,27 @@ FP8X4 = mybir.dt.float8_e4m3fn_x4
 MULT = mybir.AluOpType.mult
 ADD = mybir.AluOpType.add
 
-STEPS = [[0,1408],[1536,1024],[0,1024,"ss"],[1024,256,"s"],[1280,128,"s"],[2560,768],[1536,1024,"ss"],[3328,512],[2560,512,"s"],[3072,256,"s"],[3840,256],[1408,128],[3328,512,"ss"],[3840,256,"s"],[1408,128,"v"]]
-GATE_PIECES = [160,480,896,1024,1536]
-PAD = 416
+CHUNKS = [2048,1152,512,256,128]
+UNITS = [128,1024,1024,1024,256,256,256,128]
+LAGS = [1,1,1,2,1]
+BANKS = [128,512,512,512,512,512,512,256,256,256,128]
+GATE_PIECES = [192,576,1280,1024,896,128]
+PAD = 1056
 HALF = 512
+TURN = CHUNKS[-1]
 SPLIT = 320
+
+
+def starts(widths):
+    return [sum(widths[:i]) for i in range(len(widths) + 1)]
+
+
+def slot(place):
+    return (place + TURN) % SLOTS
+
+
+def slots(start, stop, per=1):
+    return slice(slot(start) // per, (slot(start) + stop - start) // per)
 
 
 def tile_moe_pre_lin_none_kernel(
@@ -39,9 +56,10 @@ def tile_moe_pre_lin_none_kernel(
         pos_lists = [keep.tile([P, T // 16], U16, name=f"pos_list{r}") for r in range(4)]
         x_rows = [keep.tile([P, T + PAD], F32, name=f"x_rows{j}") for j in range(PACK)]
         gate_all = keep.tile([P, SLOTS], F32, name="gate_all")
-        gate_starts = [sum(GATE_PIECES[:i]) for i in range(len(GATE_PIECES))]
+        gate_starts = starts(GATE_PIECES)
         w_codes = keep.tile([P, E, N * PACK], U8, name="w_codes", align_bytes=64)
         w_plane = keep.tile([P, E, N], U8, name="w_plane", align_bytes=64)
+        grouped = keep.tile([P, SLOTS * PACK], BF16, name="grouped", align_bytes=64)
         y = keep.tile([P, SLOTS], F32, name="y")
 
         x_by_row = xT.rearrange("(p j) t -> j p t", j=PACK)
@@ -49,9 +67,9 @@ def tile_moe_pre_lin_none_kernel(
         words_hbm = w_words.rearrange("e a p n r -> p (e a) (n r)").bitcast(I32)
         scales_hbm = w_scales.rearrange("e a q n -> q (e a) n").bitcast(I32)
 
-        def load_gate(i, queue=nc.sync):
-            cols = slice(gate_starts[i], gate_starts[i] + GATE_PIECES[i])
-            queue.dma_start(gate_all[:, cols], gate_rows[:, cols])
+        def load_gate(i):
+            cols = slots(gate_starts[i], gate_starts[i + 1])
+            nc.sync.dma_start(gate_all[:, cols], gate_rows[:, cols])
 
         def load_x(j):
             nc.sync.dma_start(x_rows[j][:, :T], x_by_row[j])
@@ -71,65 +89,71 @@ def tile_moe_pre_lin_none_kernel(
             )
         nc.sync.dma_start(w_codes[:, : E // 2, :].bitcast(I32), words_hbm[:, : E // 2, :])
         nc.sync.dma_start(w_codes[:, E // 2 :, :].bitcast(I32), words_hbm[:, E // 2 :, :])
-        load_gate(4)
+        for i in range(4, len(GATE_PIECES)):
+            load_gate(i)
         for tile, pos in zip(pos_lists, (pos1, pos2, pos3, pos4)):
             nc.sync.dma_start(tile[:], pos)
 
-        def gather(start, n):
+        def gather(start, stop):
+            n = stop - start
             prod = ring.tile([P, PACK, n], F32, name="prod")
             for j in range(PACK):
-                cuts = [s for s in gate_starts if start < s < start + n] if j == 0 else []
-                for s0, s1 in zip([start] + cuts, cuts + [start + n]):
+                cuts = [s for s in gate_starts if start < s < stop] if (j == 0 and start == 0) else []
+                for s0, s1 in zip([start] + cuts, cuts + [stop]):
                     nc.vector.tensor_tensor(
                         prod[:, j, s0 - start : s1 - start],
-                        x_rows[j][:].indirect(slot_list[:, s0 // 16 : s1 // 16]),
-                        gate_all[:, s0:s1],
+                        x_rows[j][:].indirect(slot_list[:, slots(s0, s1, 16)]),
+                        gate_all[:, slots(s0, s1)],
                         MULT,
                     )
-            grouped = keep.tile([P, n, PACK], BF16, name=f"grouped{start}", align_bytes=64)
             nc.scalar.copy(
-                out=grouped[:].rearrange("p (c i) j -> p c j i", i=4),
+                out=grouped[:, PACK * start : PACK * stop].rearrange("p (c i j) -> p c j i", i=4, j=PACK),
                 in_=prod[:].rearrange("p j (c i) -> p c j i", i=4),
             )
-            return grouped
 
-        def multiply(start, n, engines):
-            chunk = max(s for s in groups if s <= start)
+        bank_starts = starts(BANKS)
+        banks = {}
+
+        def multiply(start, stop):
+            n = stop - start
             codes = keep.tile([P, n], U32, name=f"codes{start}", align_bytes=64)
             plane = keep.tile([P, n], U8, name=f"plane{start}", align_bytes=64)
             nc.vector.quantize_mx(
-                out=codes[:].bitcast(FP8X4),
-                scales=plane[:],
-                in_=groups[chunk][:, start - chunk : start - chunk + n, :].rearrange("p c j -> p (c j)"),
+                out=codes[:].bitcast(FP8X4), scales=plane[:], in_=grouped[:, PACK * start : PACK * stop]
             )
-            width = min(n, C)
-            cols = n // len(engines)
-            for b, engine in enumerate(engines):
-                b0 = b * cols
-                acc = psum.tile([P, 512], F32, name="acc")
-                for c0 in range(b0, b0 + cols, min(width, cols)):
-                    e = (start + c0) // C
-                    w = min(width, cols)
-                    nc.tensor.matmul_mx(
-                        out=acc[:, c0 - b0 : c0 - b0 + w],
-                        lhsT=w_codes[:, e, :].bitcast(FP8X4),
-                        lhsT_scale=w_plane[:, e, :],
-                        rhs=codes[:, c0 : c0 + w].bitcast(FP8X4),
-                        rhs_scale=plane[:, c0 : c0 + w],
-                        start=True,
-                        stop=True,
-                    )
-                if engine == "v":
-                    nc.vector.tensor_copy(out=y[:, start + b0 : start + b0 + cols], in_=acc[:, :cols])
-                else:
-                    nc.scalar.copy(out=y[:, start + b0 : start + b0 + cols], in_=acc[:, :cols])
+            edges = sorted({start, stop} | {s for s in range(start, stop) if slot(s) % C == 0 or s in bank_starts})
+            for s0, s1 in zip(edges, edges[1:]):
+                b0 = max(s for s in bank_starts if s <= s0)
+                if b0 not in banks:
+                    banks[b0] = psum.tile([P, BANK], F32, name="acc")
+                nc.tensor.matmul_mx(
+                    out=banks[b0][:, s0 - b0 : s1 - b0],
+                    lhsT=w_codes[:, slot(s0) // C, :].bitcast(FP8X4),
+                    lhsT_scale=w_plane[:, slot(s0) // C, :],
+                    rhs=codes[:, s0 - start : s1 - start].bitcast(FP8X4),
+                    rhs_scale=plane[:, s0 - start : s1 - start],
+                    start=True,
+                    stop=True,
+                )
 
-        groups = {}
-        for step in STEPS:
-            if len(step) == 2:
-                groups[step[0]] = gather(*step)
+        def empty(bank):
+            b0, b1 = bank_starts[bank], bank_starts[bank + 1]
+            if b1 == SLOTS:
+                nc.vector.tensor_copy(out=y[:, slots(b0, b1)], in_=banks[b0][:, : b1 - b0])
             else:
-                multiply(*step)
+                nc.scalar.copy(out=y[:, slots(b0, b1)], in_=banks[b0][:, : b1 - b0])
+
+        chunk_starts, unit_starts = starts(CHUNKS), starts(UNITS)
+        unit, bank = 0, 0
+        for i in range(len(CHUNKS)):
+            gather(chunk_starts[i], chunk_starts[i + 1])
+            woven = chunk_starts[max(i + 1 - LAGS[i], 0)] if i + 1 < len(CHUNKS) else SLOTS
+            while unit < len(UNITS) and unit_starts[unit + 1] <= woven:
+                multiply(unit_starts[unit], unit_starts[unit + 1])
+                unit = unit + 1
+                while bank < len(BANKS) and bank_starts[bank + 1] <= unit_starts[unit]:
+                    empty(bank)
+                    bank = bank + 1
 
         def picked(r, cols):
             return y[:].indirect(pos_lists[r][:, cols.start // 16 : cols.stop // 16])

@@ -24,7 +24,7 @@ CHUNKS = [2048,1152,512,256,128]
 UNITS = [128,1024,1024,1024,256,256,256,128]
 LAGS = [1,1,1,2,1]
 BANKS = [128,512,512,512,512,512,512,256,256,256,128]
-GATE_PIECES = [192,576,1280,1024,896,128]
+GATE_PIECES = [128,256,512,1152,1024,896,128]
 PAD = 1056
 HALF = 512
 TURN = CHUNKS[-1]
@@ -77,19 +77,18 @@ def tile_moe_pre_lin_none_kernel(
         nc.vector.memset(w_plane[:].bitcast(I32), 0)
         load_x(0)
         nc.sync.dma_start(slot_list[:], offs)
-        load_gate(0)
-        load_gate(1)
-        load_gate(2)
+        for i in range(4):
+            load_gate(i)
         for j in range(1, PACK):
             load_x(j)
-        load_gate(3)
+        load_gate(4)
         for quad in range(4):
             nc.sync.dma_start(
                 w_plane[32 * quad : 32 * quad + 4, :, :].bitcast(I32), scales_hbm[4 * quad : 4 * quad + 4]
             )
         nc.sync.dma_start(w_codes[:, : E // 2, :].bitcast(I32), words_hbm[:, : E // 2, :])
         nc.sync.dma_start(w_codes[:, E // 2 :, :].bitcast(I32), words_hbm[:, E // 2 :, :])
-        for i in range(4, len(GATE_PIECES)):
+        for i in range(5, len(GATE_PIECES)):
             load_gate(i)
         for tile, pos in zip(pos_lists, (pos1, pos2, pos3, pos4)):
             nc.sync.dma_start(tile[:], pos)
@@ -166,6 +165,6 @@ def tile_moe_pre_lin_none_kernel(
             for cols in halves:
                 nc.vector.tensor_tensor(sums[r][:, cols], picked(r, cols), sums[r - 1][:, cols], ADD)
         last = [slice(0, HALF), slice(HALF, HALF + SPLIT), slice(HALF + SPLIT, T)]
-        for cols, queue in zip(last, (nc.sync, nc.scalar, nc.sync)):
+        for cols, queue in zip(last, (nc.sync, nc.sync, nc.scalar)):
             nc.vector.tensor_tensor(sums[3][:, cols], picked(3, cols), sums[2][:, cols], ADD)
             queue.dma_start(out[:, cols], sums[3][:, cols])

@@ -3,12 +3,14 @@ from contextlib import ExitStack
 import concourse.mybir as mybir
 
 K, T, E, C, N = 512, 1024, 16, 256, 128
+TOP = 4
 SLOTS = E * C
 P = 128
 PACK = 4
+PER_COLUMN = 16
 BANK = 512
 FLOPS = 2 * K * N * SLOTS
-BYTES = 4 * K * T + E * K * N + E * 16 * N + 4 * SLOTS + 2 * P * (SLOTS + 4 * T) // 16 + 4 * N * T
+BYTES = 4 * K * T + E * K * N + E * 16 * N + 4 * SLOTS + 2 * P * (SLOTS + TOP * T) // PER_COLUMN + 4 * N * T
 
 F32 = mybir.dt.float32
 BF16 = mybir.dt.bfloat16
@@ -20,15 +22,22 @@ FP8X4 = mybir.dt.float8_e4m3fn_x4
 MULT = mybir.AluOpType.mult
 ADD = mybir.AluOpType.add
 
-CHUNKS = [2048,1152,512,256,128]
-UNITS = [128,1024,1024,1024,256,256,256,128]
-LAGS = [1,1,1,2,1]
-BANKS = [128,512,512,512,512,512,512,256,256,256,128]
-GATE_PIECES = [128,256,512,1152,1024,896,128]
-PAD = 1056
-HALF = 512
-TURN = CHUNKS[-1]
-SPLIT = 320
+LAST = C // 2
+TAPER = [2 * C, C, LAST]
+FIRST = 8 * C
+CHUNKS = [FIRST, SLOTS - FIRST - sum(TAPER)] + TAPER
+
+WIDE = 4096 // PACK
+AHEAD = SLOTS - sum(TAPER)
+UNITS = [C - LAST] + [WIDE] * (AHEAD // WIDE) + [C] * ((sum(TAPER) - LAST) // C) + [LAST]
+
+GATE_HEAD = [128, 256, 512, FIRST - 128 - 256 - 512]
+GATE_PIECES = GATE_HEAD + [SLOTS - FIRST - LAST, LAST]
+
+WINDOW = FIRST + 32
+
+HALF = T // 2
+TAIL = 192
 
 
 def starts(widths):
@@ -36,7 +45,7 @@ def starts(widths):
 
 
 def slot(place):
-    return (place + TURN) % SLOTS
+    return (place + LAST) % SLOTS
 
 
 def slots(start, stop, per=1):
@@ -52,20 +61,20 @@ def tile_moe_pre_lin_none_kernel(
         ring = ctx.enter_context(tc.tile_pool(name="ring", bufs=2))
         psum = ctx.enter_context(tc.psum_pool(name="psum", bufs=8))
 
-        slot_list = keep.tile([P, SLOTS // 16], U16, name="slot_list")
-        pos_lists = [keep.tile([P, T // 16], U16, name=f"pos_list{r}") for r in range(4)]
-        x_rows = [keep.tile([P, T + PAD], F32, name=f"x_rows{j}") for j in range(PACK)]
+        slot_list = keep.tile([P, SLOTS // PER_COLUMN], U16, name="slot_list")
+        pos_lists = [keep.tile([P, T // PER_COLUMN], U16, name=f"pos_list{r}") for r in range(TOP)]
+        x_rows = [keep.tile([P, WINDOW], F32, name=f"x_rows{j}") for j in range(PACK)]
         gate_all = keep.tile([P, SLOTS], F32, name="gate_all")
-        gate_starts = starts(GATE_PIECES)
         w_codes = keep.tile([P, E, N * PACK], U8, name="w_codes", align_bytes=64)
-        w_plane = keep.tile([P, E, N], U8, name="w_plane", align_bytes=64)
-        grouped = keep.tile([P, SLOTS * PACK], BF16, name="grouped", align_bytes=64)
+        w_scale_rows = keep.tile([P, E, N], U8, name="w_scale_rows", align_bytes=64)
+        woven = keep.tile([P, SLOTS * PACK], BF16, name="woven", align_bytes=64)
         y = keep.tile([P, SLOTS], F32, name="y")
 
         x_by_row = xT.rearrange("(p j) t -> j p t", j=PACK)
         gate_rows = gate.rearrange("(p j) s -> j p s", j=PACK)[0]
         words_hbm = w_words.rearrange("e a p n r -> p (e a) (n r)").bitcast(I32)
         scales_hbm = w_scales.rearrange("e a q n -> q (e a) n").bitcast(I32)
+        gate_starts = starts(GATE_PIECES)
 
         def load_gate(i):
             cols = slots(gate_starts[i], gate_starts[i + 1])
@@ -74,97 +83,92 @@ def tile_moe_pre_lin_none_kernel(
         def load_x(j):
             nc.sync.dma_start(x_rows[j][:, :T], x_by_row[j])
 
-        nc.vector.memset(w_plane[:].bitcast(I32), 0)
+        nc.vector.memset(w_scale_rows[:].bitcast(I32), 0)
         load_x(0)
         nc.sync.dma_start(slot_list[:], offs)
-        for i in range(4):
+        for i in range(len(GATE_HEAD)):
             load_gate(i)
         for j in range(1, PACK):
             load_x(j)
-        load_gate(4)
+        load_gate(len(GATE_HEAD))
         for quad in range(4):
             nc.sync.dma_start(
-                w_plane[32 * quad : 32 * quad + 4, :, :].bitcast(I32), scales_hbm[4 * quad : 4 * quad + 4]
+                w_scale_rows[32 * quad : 32 * quad + 4, :, :].bitcast(I32), scales_hbm[4 * quad : 4 * quad + 4]
             )
-        nc.sync.dma_start(w_codes[:, : E // 2, :].bitcast(I32), words_hbm[:, : E // 2, :])
-        nc.sync.dma_start(w_codes[:, E // 2 :, :].bitcast(I32), words_hbm[:, E // 2 :, :])
-        for i in range(5, len(GATE_PIECES)):
+        for experts in (slice(0, E // 2), slice(E // 2, E)):
+            nc.sync.dma_start(w_codes[:, experts, :].bitcast(I32), words_hbm[:, experts, :])
+        for i in range(len(GATE_HEAD) + 1, len(GATE_PIECES)):
             load_gate(i)
         for tile, pos in zip(pos_lists, (pos1, pos2, pos3, pos4)):
             nc.sync.dma_start(tile[:], pos)
 
-        def gather(start, stop):
-            n = stop - start
-            prod = ring.tile([P, PACK, n], F32, name="prod")
+        def gather_and_weave(start, stop):
+            prod = ring.tile([P, PACK, stop - start], F32, name="prod")
             for j in range(PACK):
-                cuts = [s for s in gate_starts if start < s < stop] if (j == 0 and start == 0) else []
-                for s0, s1 in zip([start] + cuts, cuts + [stop]):
+                edges = starts(GATE_HEAD) if (start, j) == (0, 0) else [start, stop]
+                for s0, s1 in zip(edges, edges[1:]):
                     nc.vector.tensor_tensor(
                         prod[:, j, s0 - start : s1 - start],
-                        x_rows[j][:].indirect(slot_list[:, slots(s0, s1, 16)]),
+                        x_rows[j][:].indirect(slot_list[:, slots(s0, s1, PER_COLUMN)]),
                         gate_all[:, slots(s0, s1)],
                         MULT,
                     )
             nc.scalar.copy(
-                out=grouped[:, PACK * start : PACK * stop].rearrange("p (c i j) -> p c j i", i=4, j=PACK),
+                out=woven[:, PACK * start : PACK * stop].rearrange("p (c i j) -> p c j i", i=4, j=PACK),
                 in_=prod[:].rearrange("p j (c i) -> p c j i", i=4),
             )
 
-        bank_starts = starts(BANKS)
-        banks = {}
-
-        def multiply(start, stop):
+        def quantise_and_multiply(start, stop):
             n = stop - start
             codes = keep.tile([P, n], U32, name=f"codes{start}", align_bytes=64)
-            plane = keep.tile([P, n], U8, name=f"plane{start}", align_bytes=64)
+            scale_rows = keep.tile([P, n], U8, name=f"scale_rows{start}", align_bytes=64)
             nc.vector.quantize_mx(
-                out=codes[:].bitcast(FP8X4), scales=plane[:], in_=grouped[:, PACK * start : PACK * stop]
+                out=codes[:].bitcast(FP8X4), scales=scale_rows[:], in_=woven[:, PACK * start : PACK * stop]
             )
-            edges = sorted({start, stop} | {s for s in range(start, stop) if slot(s) % C == 0 or s in bank_starts})
-            for s0, s1 in zip(edges, edges[1:]):
-                b0 = max(s for s in bank_starts if s <= s0)
-                if b0 not in banks:
-                    banks[b0] = psum.tile([P, BANK], F32, name="acc")
-                nc.tensor.matmul_mx(
-                    out=banks[b0][:, s0 - b0 : s1 - b0],
-                    lhsT=w_codes[:, slot(s0) // C, :].bitcast(FP8X4),
-                    lhsT_scale=w_plane[:, slot(s0) // C, :],
-                    rhs=codes[:, s0 - start : s1 - start].bitcast(FP8X4),
-                    rhs_scale=plane[:, s0 - start : s1 - start],
-                    start=True,
-                    stop=True,
-                )
-
-        def empty(bank):
-            b0, b1 = bank_starts[bank], bank_starts[bank + 1]
-            if b1 == SLOTS:
-                nc.vector.tensor_copy(out=y[:, slots(b0, b1)], in_=banks[b0][:, : b1 - b0])
-            else:
-                nc.scalar.copy(out=y[:, slots(b0, b1)], in_=banks[b0][:, : b1 - b0])
+            filled = []
+            for b0 in range(0, n, BANK):
+                acc = psum.tile([P, BANK], F32, name="acc")
+                width = min(n, BANK)
+                for c0 in range(b0, b0 + width, C):
+                    cols = slice(c0, min(c0 + C, n))
+                    expert = slot(start + c0) // C
+                    nc.tensor.matmul_mx(
+                        out=acc[:, cols.start - b0 : cols.stop - b0],
+                        lhsT=w_codes[:, expert, :].bitcast(FP8X4),
+                        lhsT_scale=w_scale_rows[:, expert, :],
+                        rhs=codes[:, cols].bitcast(FP8X4),
+                        rhs_scale=scale_rows[:, cols],
+                        start=True,
+                        stop=True,
+                    )
+                filled.append((y[:, slots(start + b0, start + b0 + width)], acc[:, :width]))
+            for results, sums in filled:
+                if stop == SLOTS:
+                    nc.vector.tensor_copy(out=results, in_=sums)
+                else:
+                    nc.scalar.copy(out=results, in_=sums)
 
         chunk_starts, unit_starts = starts(CHUNKS), starts(UNITS)
-        unit, bank = 0, 0
-        for i in range(len(CHUNKS)):
-            gather(chunk_starts[i], chunk_starts[i + 1])
-            woven = chunk_starts[max(i + 1 - LAGS[i], 0)] if i + 1 < len(CHUNKS) else SLOTS
-            while unit < len(UNITS) and unit_starts[unit + 1] <= woven:
-                multiply(unit_starts[unit], unit_starts[unit + 1])
-                unit = unit + 1
-                while bank < len(BANKS) and bank_starts[bank + 1] <= unit_starts[unit]:
-                    empty(bank)
-                    bank = bank + 1
+        done = 0
+        for start, stop in zip(chunk_starts, chunk_starts[1:]):
+            gather_and_weave(start, stop)
+            ready = SLOTS if stop == SLOTS else min(start, AHEAD)
+            for u0, u1 in zip(unit_starts, unit_starts[1:]):
+                if done <= u0 and u1 <= ready:
+                    quantise_and_multiply(u0, u1)
+                    done = u1
 
-        def picked(r, cols):
-            return y[:].indirect(pos_lists[r][:, cols.start // 16 : cols.stop // 16])
+        def picked(r, tokens):
+            return y[:].indirect(pos_lists[r][:, tokens.start // PER_COLUMN : tokens.stop // PER_COLUMN])
 
-        sums = [keep.tile([P, T], F32, name=f"sum{r}") for r in range(4)]
+        totals = [keep.tile([P, T], F32, name=f"total{r}") for r in range(TOP)]
         halves = [slice(0, HALF), slice(HALF, T)]
-        for cols in halves:
-            nc.vector.tensor_copy(sums[0][:, cols], picked(0, cols))
-        for r in (1, 2):
-            for cols in halves:
-                nc.vector.tensor_tensor(sums[r][:, cols], picked(r, cols), sums[r - 1][:, cols], ADD)
-        last = [slice(0, HALF), slice(HALF, HALF + SPLIT), slice(HALF + SPLIT, T)]
-        for cols, queue in zip(last, (nc.sync, nc.sync, nc.scalar)):
-            nc.vector.tensor_tensor(sums[3][:, cols], picked(3, cols), sums[2][:, cols], ADD)
-            queue.dma_start(out[:, cols], sums[3][:, cols])
+        for tokens in halves:
+            nc.vector.tensor_copy(totals[0][:, tokens], picked(0, tokens))
+        for r in range(1, TOP - 1):
+            for tokens in halves:
+                nc.vector.tensor_tensor(totals[r][:, tokens], picked(r, tokens), totals[r - 1][:, tokens], ADD)
+        parts = [slice(0, HALF), slice(HALF, T - TAIL), slice(T - TAIL, T)]
+        for tokens, queue in zip(parts, (nc.sync, nc.scalar, nc.sync)):
+            nc.vector.tensor_tensor(totals[-1][:, tokens], picked(TOP - 1, tokens), totals[-2][:, tokens], ADD)
+            queue.dma_start(out[:, tokens], totals[-1][:, tokens])

@@ -84,9 +84,10 @@ def tile_moe_pre_lin_none_kernel(
             nc.sync.dma_start(x_rows[j][:, :T], x_by_row[j])
 
         nc.vector.memset(w_scale_rows[:].bitcast(I32), 0)
-        load_x(0)
         nc.sync.dma_start(slot_list[:], offs)
-        for i in range(len(GATE_HEAD)):
+        load_gate(0)
+        load_x(0)
+        for i in range(1, len(GATE_HEAD)):
             load_gate(i)
         for j in range(1, PACK):
             load_x(j)
@@ -143,10 +144,7 @@ def tile_moe_pre_lin_none_kernel(
                     )
                 filled.append((y[:, slots(start + b0, start + b0 + width)], acc[:, :width]))
             for results, sums in filled:
-                if stop == SLOTS:
-                    nc.vector.tensor_copy(out=results, in_=sums)
-                else:
-                    nc.scalar.copy(out=results, in_=sums)
+                nc.scalar.copy(out=results, in_=sums)
 
         chunk_starts, unit_starts = starts(CHUNKS), starts(UNITS)
         done = 0

@@ -1,6 +1,7 @@
 from contextlib import ExitStack
 
 import concourse.mybir as mybir
+from concourse.masks import make_identity
 
 K, T, E, C, N = 512, 1024, 16, 256, 128
 TOP = 4
@@ -21,6 +22,7 @@ U8 = mybir.dt.uint8
 FP8X4 = mybir.dt.float8_e4m3fn_x4
 MULT = mybir.AluOpType.mult
 ADD = mybir.AluOpType.add
+COPY = mybir.ActivationFunctionType.Copy
 
 LAST = C // 2
 TAPER = [2 * C, C, LAST]
@@ -31,8 +33,8 @@ WIDE = 4096 // PACK
 AHEAD = SLOTS - sum(TAPER)
 UNITS = [C - LAST] + [WIDE] * (AHEAD // WIDE) + [C] * ((sum(TAPER) - LAST) // C) + [LAST]
 
-GATE_HEAD = [128, 256, 512, FIRST - 128 - 256 - 512]
-GATE_PIECES = GATE_HEAD + [SLOTS - FIRST - LAST, LAST]
+TURNED = 1
+GATE_PIECES = [FIRST // 2, FIRST // 2, SLOTS - FIRST - LAST, LAST]
 
 WINDOW = FIRST + 32
 
@@ -59,6 +61,7 @@ def tile_moe_pre_lin_none_kernel(
     with ExitStack() as ctx:
         keep = ctx.enter_context(tc.tile_pool(name="keep", bufs=1))
         ring = ctx.enter_context(tc.tile_pool(name="ring", bufs=2))
+        stage = ctx.enter_context(tc.tile_pool(name="stage", bufs=2))
         psum = ctx.enter_context(tc.psum_pool(name="psum", bufs=8))
 
         slot_list = keep.tile([P, SLOTS // PER_COLUMN], U16, name="slot_list")
@@ -69,6 +72,12 @@ def tile_moe_pre_lin_none_kernel(
         w_scale_rows = keep.tile([P, E, N], U8, name="w_scale_rows", align_bytes=64)
         woven = keep.tile([P, SLOTS * PACK], BF16, name="woven", align_bytes=64)
         y = keep.tile([P, SLOTS], F32, name="y")
+
+        plain = [keep.tile([P, FIRST], F32, name=f"plain{j}") for j in range(TURNED)]
+        gate_blocks = keep.tile([P, P], F32, name="gate_blocks")
+        gate_columns = keep.tile([P, SLOTS // P], F32, name="gate_columns")
+        identity = keep.tile([P, P], F32, name="identity")
+        make_identity(nc, identity[:])
 
         x_by_row = xT.rearrange("(p j) t -> j p t", j=PACK)
         gate_rows = gate.rearrange("(p j) s -> j p s", j=PACK)[0]
@@ -85,35 +94,54 @@ def tile_moe_pre_lin_none_kernel(
 
         nc.vector.memset(w_scale_rows[:].bitcast(I32), 0)
         nc.sync.dma_start(slot_list[:], offs)
-        load_gate(0)
         load_x(0)
-        for i in range(1, len(GATE_HEAD)):
-            load_gate(i)
-        for j in range(1, PACK):
+        load_x(1)
+        load_gate(0)
+        load_gate(1)
+        nc.sync.dma_start(gate_blocks[:], gate.rearrange("k (b c) -> (k b) c", c=P)[:P, :])
+        for j in range(2, PACK):
             load_x(j)
-        load_gate(len(GATE_HEAD))
+        load_gate(2)
         for quad in range(4):
             nc.sync.dma_start(
                 w_scale_rows[32 * quad : 32 * quad + 4, :, :].bitcast(I32), scales_hbm[4 * quad : 4 * quad + 4]
             )
         for experts in (slice(0, E // 2), slice(E // 2, E)):
             nc.sync.dma_start(w_codes[:, experts, :].bitcast(I32), words_hbm[:, experts, :])
-        for i in range(len(GATE_HEAD) + 1, len(GATE_PIECES)):
-            load_gate(i)
+        load_gate(3)
         for tile, pos in zip(pos_lists, (pos1, pos2, pos3, pos4)):
             nc.sync.dma_start(tile[:], pos)
+
+        turned_gate = psum.tile([P, BANK], F32, name="acc")
+        nc.tensor.transpose(turned_gate[:, :P], gate_blocks[:], identity[:])
+        nc.scalar.copy(out=gate_columns[:], in_=turned_gate[:, : SLOTS // P])
+
+        def times_gate(products, values):
+            for b0 in range(0, FIRST, BANK):
+                turned = psum.tile([P, BANK], F32, name="acc")
+                scaled = stage.tile([P, BANK], F32, name="scaled")
+                back = psum.tile([P, BANK], F32, name="acc")
+                blocks = [slice(c0, c0 + P) for c0 in range(0, BANK, P)]
+                for cols in blocks:
+                    nc.tensor.transpose(turned[:, cols], values[:, b0 + cols.start : b0 + cols.stop], identity[:])
+                for cols in blocks:
+                    block = slot(b0 + cols.start) // P
+                    nc.scalar.activation(
+                        scaled[:, cols], turned[:, cols], COPY, scale=gate_columns[:, block : block + 1]
+                    )
+                for cols in blocks:
+                    nc.tensor.transpose(back[:, cols], scaled[:, cols], identity[:])
+                nc.scalar.copy(out=products[:, b0 : b0 + BANK], in_=back[:])
 
         def gather_and_weave(start, stop):
             prod = ring.tile([P, PACK, stop - start], F32, name="prod")
             for j in range(PACK):
-                edges = starts(GATE_HEAD) if (start, j) == (0, 0) else [start, stop]
-                for s0, s1 in zip(edges, edges[1:]):
-                    nc.vector.tensor_tensor(
-                        prod[:, j, s0 - start : s1 - start],
-                        x_rows[j][:].indirect(slot_list[:, slots(s0, s1, PER_COLUMN)]),
-                        gate_all[:, slots(s0, s1)],
-                        MULT,
-                    )
+                picked_x = x_rows[j][:].indirect(slot_list[:, slots(start, stop, PER_COLUMN)])
+                if start == 0 and j < TURNED:
+                    nc.vector.tensor_copy(plain[j][:], picked_x)
+                    times_gate(prod[:, j, :], plain[j])
+                else:
+                    nc.vector.tensor_tensor(prod[:, j, :], picked_x, gate_all[:, slots(start, stop)], MULT)
             nc.scalar.copy(
                 out=woven[:, PACK * start : PACK * stop].rearrange("p (c i j) -> p c j i", i=4, j=PACK),
                 in_=prod[:].rearrange("p j (c i) -> p c j i", i=4),

@@ -143,8 +143,8 @@ def tile_moe_pre_lin_none_kernel(
                 else:
                     nc.vector.tensor_tensor(prod[:, j, :], picked_x, gate_all[:, slots(start, stop)], MULT)
             nc.scalar.copy(
-                out=woven[:, PACK * start : PACK * stop].rearrange("p (c i j) -> p c j i", i=4, j=PACK),
-                in_=prod[:].rearrange("p j (c i) -> p c j i", i=4),
+                out=woven[:, PACK * start : PACK * stop].rearrange("p (c i j) -> p c j i", i=2, j=PACK),
+                in_=prod[:].rearrange("p j (c i) -> p c j i", i=2),
             )
 
         def quantise_and_multiply(start, stop):

@@ -33,7 +33,6 @@ WIDE = 4096 // PACK
 AHEAD = SLOTS - sum(TAPER)
 UNITS = [C - LAST] + [WIDE] * (AHEAD // WIDE) + [C] * ((sum(TAPER) - LAST) // C) + [LAST]
 
-TURNED = 1
 GATE_PIECES = [FIRST // 2, FIRST // 2, SLOTS - FIRST - LAST, LAST]
 
 WINDOW = FIRST + 32
@@ -73,14 +72,15 @@ def tile_moe_pre_lin_none_kernel(
         woven = keep.tile([P, SLOTS * PACK], BF16, name="woven", align_bytes=64)
         y = keep.tile([P, SLOTS], F32, name="y")
 
-        plain = [keep.tile([P, FIRST], F32, name=f"plain{j}") for j in range(TURNED)]
+        first_picked = keep.tile([P, FIRST], F32, name="first_picked")
         gate_blocks = keep.tile([P, P], F32, name="gate_blocks")
-        gate_columns = keep.tile([P, SLOTS // P], F32, name="gate_columns")
+        gate_columns = keep.tile([P, FIRST // P], F32, name="gate_columns")
         identity = keep.tile([P, P], F32, name="identity")
         make_identity(nc, identity[:])
 
         x_by_row = xT.rearrange("(p j) t -> j p t", j=PACK)
         gate_rows = gate.rearrange("(p j) s -> j p s", j=PACK)[0]
+        blocks_hbm = gate.rearrange("k (b c) -> (k b) c", c=P)[LAST // P : LAST // P + P, :]
         words_hbm = w_words.rearrange("e a p n r -> p (e a) (n r)").bitcast(I32)
         scales_hbm = w_scales.rearrange("e a q n -> q (e a) n").bitcast(I32)
         gate_starts = starts(GATE_PIECES)
@@ -98,7 +98,7 @@ def tile_moe_pre_lin_none_kernel(
         load_x(1)
         load_gate(0)
         load_gate(1)
-        nc.sync.dma_start(gate_blocks[:], gate.rearrange("k (b c) -> (k b) c", c=P)[:P, :])
+        nc.sync.dma_start(gate_blocks[:], blocks_hbm)
         for j in range(2, PACK):
             load_x(j)
         load_gate(2)
@@ -114,7 +114,7 @@ def tile_moe_pre_lin_none_kernel(
 
         turned_gate = psum.tile([P, BANK], F32, name="acc")
         nc.tensor.transpose(turned_gate[:, :P], gate_blocks[:], identity[:])
-        nc.scalar.copy(out=gate_columns[:], in_=turned_gate[:, : SLOTS // P])
+        nc.scalar.copy(out=gate_columns[:], in_=turned_gate[:, : FIRST // P])
 
         def times_gate(products, values):
             for b0 in range(0, FIRST, BANK):
@@ -125,7 +125,7 @@ def tile_moe_pre_lin_none_kernel(
                 for cols in blocks:
                     nc.tensor.transpose(turned[:, cols], values[:, b0 + cols.start : b0 + cols.stop], identity[:])
                 for cols in blocks:
-                    block = slot(b0 + cols.start) // P
+                    block = (b0 + cols.start) // P
                     nc.scalar.activation(
                         scaled[:, cols], turned[:, cols], COPY, scale=gate_columns[:, block : block + 1]
                     )
@@ -137,9 +137,9 @@ def tile_moe_pre_lin_none_kernel(
             prod = ring.tile([P, PACK, stop - start], F32, name="prod")
             for j in range(PACK):
                 picked_x = x_rows[j][:].indirect(slot_list[:, slots(start, stop, PER_COLUMN)])
-                if start == 0 and j < TURNED:
-                    nc.vector.tensor_copy(plain[j][:], picked_x)
-                    times_gate(prod[:, j, :], plain[j])
+                if (start, j) == (0, 0):
+                    nc.vector.tensor_copy(first_picked[:], picked_x)
+                    times_gate(prod[:, j, :], first_picked)
                 else:
                     nc.vector.tensor_tensor(prod[:, j, :], picked_x, gate_all[:, slots(start, stop)], MULT)
             nc.scalar.copy(

@@ -1,7 +1,6 @@
 from contextlib import ExitStack
 
 import concourse.mybir as mybir
-from concourse.masks import make_identity
 
 K, T, E, C, N = 512, 1024, 16, 256, 128
 TOP = 4
@@ -24,33 +23,21 @@ MULT = mybir.AluOpType.mult
 ADD = mybir.AluOpType.add
 COPY = mybir.ActivationFunctionType.Copy
 
-LAST = C // 2
-TAPER = [2 * C, C, LAST]
-FIRST = 8 * C
-CHUNKS = [FIRST, SLOTS - FIRST - sum(TAPER)] + TAPER
-
-WIDE = 4096 // PACK
-AHEAD = SLOTS - sum(TAPER)
-UNITS = [C - LAST] + [WIDE] * (AHEAD // WIDE) + [C] * ((sum(TAPER) - LAST) // C) + [LAST]
-
-GATE_PIECES = [FIRST // 2, FIRST // 2, SLOTS - FIRST - LAST, LAST]
-
-WINDOW = FIRST + 32
-
-HALF = T // 2
-TAIL = 192
+OWN = 1152
+SHARED = [1024,896,512,256,256]
+PIECES = [1024,896,512,256,128,128]
+UNITS = [1024,1024,1024,512,256,128,128]
+WINDOW = max([OWN] + SHARED) + 32
+NEAR = 2
 
 
-def starts(widths):
-    return [sum(widths[:i]) for i in range(len(widths) + 1)]
+def starts(widths, first=0):
+    return [first + sum(widths[:i]) for i in range(len(widths) + 1)]
 
 
-def slot(place):
-    return (place + LAST) % SLOTS
-
-
-def slots(start, stop, per=1):
-    return slice(slot(start) // per, (slot(start) + stop - start) // per)
+def runs(widths, first=0):
+    edges = starts(widths, first)
+    return list(zip(edges, edges[1:]))
 
 
 def tile_moe_pre_lin_none_kernel(
@@ -59,93 +46,77 @@ def tile_moe_pre_lin_none_kernel(
     nc = tc.nc
     with ExitStack() as ctx:
         keep = ctx.enter_context(tc.tile_pool(name="keep", bufs=1))
-        ring = ctx.enter_context(tc.tile_pool(name="ring", bufs=2))
-        stage = ctx.enter_context(tc.tile_pool(name="stage", bufs=2))
         psum = ctx.enter_context(tc.psum_pool(name="psum", bufs=8))
 
         slot_list = keep.tile([P, SLOTS // PER_COLUMN], U16, name="slot_list")
         pos_lists = [keep.tile([P, T // PER_COLUMN], U16, name=f"pos_list{r}") for r in range(TOP)]
         x_rows = [keep.tile([P, WINDOW], F32, name=f"x_rows{j}") for j in range(PACK)]
-        gate_all = keep.tile([P, SLOTS], F32, name="gate_all")
+        gate_own = keep.tile([P, OWN], F32, name="gate_own")
+        gate_rest = keep.tile([P, SLOTS - OWN], F32, name="gate_rest")
         w_codes = keep.tile([P, E, N * PACK], U8, name="w_codes", align_bytes=64)
         w_scale_rows = keep.tile([P, E, N], U8, name="w_scale_rows", align_bytes=64)
         woven = keep.tile([P, SLOTS * PACK], BF16, name="woven", align_bytes=64)
         y = keep.tile([P, SLOTS], F32, name="y")
 
-        first_picked = keep.tile([P, FIRST], F32, name="first_picked")
-        gate_blocks = keep.tile([P, P], F32, name="gate_blocks")
-        gate_columns = keep.tile([P, FIRST // P], F32, name="gate_columns")
-        identity = keep.tile([P, P], F32, name="identity")
-        make_identity(nc, identity[:])
-
         x_by_row = xT.rearrange("(p j) t -> j p t", j=PACK)
         gate_rows = gate.rearrange("(p j) s -> j p s", j=PACK)[0]
-        blocks_hbm = gate.rearrange("k (b c) -> (k b) c", c=P)[LAST // P : LAST // P + P, :]
         words_hbm = w_words.rearrange("e a p n r -> p (e a) (n r)").bitcast(I32)
         scales_hbm = w_scales.rearrange("e a q n -> q (e a) n").bitcast(I32)
-        gate_starts = starts(GATE_PIECES)
-
-        def load_gate(i):
-            cols = slots(gate_starts[i], gate_starts[i + 1])
-            nc.sync.dma_start(gate_all[:, cols], gate_rows[:, cols])
-
-        def load_x(j):
-            nc.sync.dma_start(x_rows[j][:, :T], x_by_row[j])
 
         nc.vector.memset(w_scale_rows[:].bitcast(I32), 0)
         nc.sync.dma_start(slot_list[:], offs)
-        load_x(0)
-        load_x(1)
-        load_gate(0)
-        load_gate(1)
-        nc.sync.dma_start(gate_blocks[:], blocks_hbm)
-        for j in range(2, PACK):
-            load_x(j)
-        load_gate(2)
+        nc.sync.dma_start(x_rows[0][:, :T], x_by_row[0])
+        nc.sync.dma_start(gate_own[:], gate_rows[:, :OWN])
+        for j in range(1, PACK):
+            nc.sync.dma_start(x_rows[j][:, :T], x_by_row[j])
+        for start, stop in runs([1024,1024,896], OWN):
+            nc.sync.dma_start(gate_rest[:, start - OWN : stop - OWN], gate_rows[:, start:stop])
         for quad in range(4):
             nc.sync.dma_start(
                 w_scale_rows[32 * quad : 32 * quad + 4, :, :].bitcast(I32), scales_hbm[4 * quad : 4 * quad + 4]
             )
         for experts in (slice(0, E // 2), slice(E // 2, E)):
             nc.sync.dma_start(w_codes[:, experts, :].bitcast(I32), words_hbm[:, experts, :])
-        load_gate(3)
         for tile, pos in zip(pos_lists, (pos1, pos2, pos3, pos4)):
             nc.sync.dma_start(tile[:], pos)
 
-        turned_gate = psum.tile([P, BANK], F32, name="acc")
-        nc.tensor.transpose(turned_gate[:, :P], gate_blocks[:], identity[:])
-        nc.scalar.copy(out=gate_columns[:], in_=turned_gate[:, : FIRST // P])
+        def picked_x(j, start, stop):
+            return x_rows[j][:].indirect(slot_list[:, start // PER_COLUMN : stop // PER_COLUMN])
 
-        def times_gate(products, values):
-            for b0 in range(0, FIRST, BANK):
-                turned = psum.tile([P, BANK], F32, name="acc")
-                scaled = stage.tile([P, BANK], F32, name="scaled")
-                back = psum.tile([P, BANK], F32, name="acc")
-                blocks = [slice(c0, c0 + P) for c0 in range(0, BANK, P)]
-                for cols in blocks:
-                    nc.tensor.transpose(turned[:, cols], values[:, b0 + cols.start : b0 + cols.stop], identity[:])
-                for cols in blocks:
-                    block = (b0 + cols.start) // P
-                    nc.scalar.activation(
-                        scaled[:, cols], turned[:, cols], COPY, scale=gate_columns[:, block : block + 1]
-                    )
-                for cols in blocks:
-                    nc.tensor.transpose(back[:, cols], scaled[:, cols], identity[:])
-                nc.scalar.copy(out=products[:, b0 : b0 + BANK], in_=back[:])
+        def woven_view(start, stop):
+            return woven[:, PACK * start : PACK * stop].rearrange("p (c i j) -> p c j i", i=NEAR, j=PACK)
 
-        def gather_and_weave(start, stop):
-            prod = ring.tile([P, PACK, stop - start], F32, name="prod")
+        pieces = runs(PIECES, OWN)
+        chunks = runs(SHARED, OWN)
+        raw = {start: keep.tile([P, PACK, stop - start], F32, name=f"raw{start}") for start, stop in chunks}
+        helped = {(3072, 0)}
+        for start, stop in chunks:
+            if (start, 0) in helped:
+                nc.vector.tensor_copy(raw[start][:, 0, :], picked_x(0, start, stop))
+        products = keep.tile([P, PACK, OWN], F32, name="products")
+        for j in range(PACK):
+            nc.vector.tensor_tensor(products[:, j, :], picked_x(j, 0, OWN), gate_own[:], MULT)
+        for start, stop in chunks:
+            if (start, 3) in helped:
+                nc.vector.tensor_copy(raw[start][:, 3, :], picked_x(3, start, stop))
+        for start, stop in chunks:
             for j in range(PACK):
-                picked_x = x_rows[j][:].indirect(slot_list[:, slots(start, stop, PER_COLUMN)])
-                if (start, j) == (0, 0):
-                    nc.vector.tensor_copy(first_picked[:], picked_x)
-                    times_gate(prod[:, j, :], first_picked)
-                else:
-                    nc.vector.tensor_tensor(prod[:, j, :], picked_x, gate_all[:, slots(start, stop)], MULT)
-            nc.scalar.copy(
-                out=woven[:, PACK * start : PACK * stop].rearrange("p (c i j) -> p c j i", i=2, j=PACK),
-                in_=prod[:].rearrange("p j (c i) -> p c j i", i=2),
+                if (start, j) not in helped:
+                    nc.scalar.activation(raw[start][:, j, :], picked_x(j, start, stop), COPY)
+        nc.vector.tensor_copy(woven_view(0, OWN), products[:].rearrange("p j (c i) -> p c j i", i=NEAR))
+
+        def times_gate_and_weave(start, stop):
+            base = max(s for s in raw if s <= start)
+            n = stop - start
+            gate_view = gate_rest[:, start - OWN : stop - OWN].rearrange("p (c i) -> p c i", i=NEAR)
+            nc.vector.tensor_tensor(
+                woven_view(start, stop),
+                raw[base][:, :, start - base : stop - base].rearrange("p j (c i) -> p c j i", i=NEAR),
+                gate_view.unsqueeze(2).to_broadcast([P, n // NEAR, PACK, NEAR]),
+                MULT,
             )
+
+        filled = []
 
         def quantise_and_multiply(start, stop):
             n = stop - start
@@ -154,13 +125,12 @@ def tile_moe_pre_lin_none_kernel(
             nc.vector.quantize_mx(
                 out=codes[:].bitcast(FP8X4), scales=scale_rows[:], in_=woven[:, PACK * start : PACK * stop]
             )
-            filled = []
             for b0 in range(0, n, BANK):
                 acc = psum.tile([P, BANK], F32, name="acc")
                 width = min(n, BANK)
                 for c0 in range(b0, b0 + width, C):
                     cols = slice(c0, min(c0 + C, n))
-                    expert = slot(start + c0) // C
+                    expert = (start + c0) // C
                     nc.tensor.matmul_mx(
                         out=acc[:, cols.start - b0 : cols.stop - b0],
                         lhsT=w_codes[:, expert, :].bitcast(FP8X4),
@@ -170,31 +140,35 @@ def tile_moe_pre_lin_none_kernel(
                         start=True,
                         stop=True,
                     )
-                filled.append((y[:, slots(start + b0, start + b0 + width)], acc[:, :width]))
-            for results, sums in filled:
-                nc.scalar.copy(out=results, in_=sums)
+                nc.scalar.copy(out=y[:, start + b0 : start + b0 + width], in_=acc[:, :width])
 
-        chunk_starts, unit_starts = starts(CHUNKS), starts(UNITS)
         done = 0
-        for start, stop in zip(chunk_starts, chunk_starts[1:]):
-            gather_and_weave(start, stop)
-            ready = SLOTS if stop == SLOTS else min(start, AHEAD)
-            for u0, u1 in zip(unit_starts, unit_starts[1:]):
-                if done <= u0 and u1 <= ready:
+        units = runs(UNITS)
+        for start, stop in pieces + [(SLOTS, SLOTS)]:
+            if start < SLOTS:
+                times_gate_and_weave(start, stop)
+            for u0, u1 in units:
+                if done <= u0 and u1 <= start:
                     quantise_and_multiply(u0, u1)
                     done = u1
 
         def picked(r, tokens):
             return y[:].indirect(pos_lists[r][:, tokens.start // PER_COLUMN : tokens.stop // PER_COLUMN])
 
+        fetched = [keep.tile([P, T], F32, name=f"fetched{r}") for r in range(3)]
         totals = [keep.tile([P, T], F32, name=f"total{r}") for r in range(TOP)]
-        halves = [slice(0, HALF), slice(HALF, T)]
-        for tokens in halves:
-            nc.vector.tensor_copy(totals[0][:, tokens], picked(0, tokens))
-        for r in range(1, TOP - 1):
-            for tokens in halves:
-                nc.vector.tensor_tensor(totals[r][:, tokens], picked(r, tokens), totals[r - 1][:, tokens], ADD)
-        parts = [slice(0, HALF), slice(HALF, T - TAIL), slice(T - TAIL, T)]
-        for tokens, queue in zip(parts, (nc.sync, nc.scalar, nc.sync)):
-            nc.vector.tensor_tensor(totals[-1][:, tokens], picked(TOP - 1, tokens), totals[-2][:, tokens], ADD)
-            queue.dma_start(out[:, tokens], totals[-1][:, tokens])
+        lead, mid, last = slice(0, 256), slice(256, 768), slice(768, T)
+        front = slice(0, last.start)
+        for r, tokens in ((0, mid), (0, last), (1, front), (0, lead), (1, last), (2, last)):
+            nc.scalar.activation(fetched[r][:, tokens], picked(r, tokens), COPY)
+        nc.vector.tensor_copy(totals[0][:, lead], picked(2, lead))
+        nc.vector.tensor_tensor(totals[1][:, lead], picked(3, lead), totals[0][:, lead], ADD)
+        nc.vector.tensor_tensor(totals[0][:, mid], picked(2, mid), fetched[0][:, mid], ADD)
+        nc.vector.tensor_tensor(totals[1][:, last], picked(3, last), fetched[0][:, last], ADD)
+        nc.vector.tensor_tensor(totals[2][:, mid], picked(3, mid), totals[0][:, mid], ADD)
+        nc.vector.tensor_tensor(totals[2][:, lead], totals[1][:, lead], fetched[0][:, lead], ADD)
+        nc.vector.tensor_tensor(totals[2][:, last], totals[1][:, last], fetched[1][:, last], ADD)
+        nc.vector.tensor_tensor(totals[3][:, front], totals[2][:, front], fetched[1][:, front], ADD)
+        nc.sync.dma_start(out[:, front], totals[3][:, front])
+        nc.vector.tensor_tensor(totals[3][:, last], totals[2][:, last], fetched[2][:, last], ADD)
+        nc.scalar.dma_start(out[:, last], totals[3][:, last])

@@ -23,9 +23,9 @@ MULT = mybir.AluOpType.mult
 ADD = mybir.AluOpType.add
 COPY = mybir.ActivationFunctionType.Copy
 
-OWN = 1152
-SHARED = [1024,896,512,256,256]
-PIECES = [1024,896,512,256,128,128]
+OWN = 1024
+SHARED = [1280,768,512,256,256]
+PIECES = [1280,768,512,256,128,128]
 UNITS = [1024,1024,1024,512,256,128,128]
 WINDOW = max([OWN] + SHARED) + 32
 NEAR = 2
@@ -51,7 +51,7 @@ def tile_moe_pre_lin_none_kernel(
         slot_list = keep.tile([P, SLOTS // PER_COLUMN], U16, name="slot_list")
         pos_lists = [keep.tile([P, T // PER_COLUMN], U16, name=f"pos_list{r}") for r in range(TOP)]
         x_rows = [keep.tile([P, WINDOW], F32, name=f"x_rows{j}") for j in range(PACK)]
-        gate_own = keep.tile([P, OWN], F32, name="gate_own")
+        gate_own = keep.tile([P, OWN], F32, name="gate_own", tag="second")
         gate_rest = keep.tile([P, SLOTS - OWN], F32, name="gate_rest")
         w_codes = keep.tile([P, E, N * PACK], U8, name="w_codes", align_bytes=64)
         w_scale_rows = keep.tile([P, E, N], U8, name="w_scale_rows", align_bytes=64)
@@ -63,13 +63,16 @@ def tile_moe_pre_lin_none_kernel(
         words_hbm = w_words.rearrange("e a p n r -> p (e a) (n r)").bitcast(I32)
         scales_hbm = w_scales.rearrange("e a q n -> q (e a) n").bitcast(I32)
 
+        warm = keep.tile([P, 2], F32, name="warm")
+        nc.gpsimd.memset(warm[:, 0:1], 0.0)
+        nc.scalar.activation(warm[:, 1:2], warm[:, 0:1], COPY)
         nc.vector.memset(w_scale_rows[:].bitcast(I32), 0)
         nc.sync.dma_start(slot_list[:], offs)
         nc.sync.dma_start(x_rows[0][:, :T], x_by_row[0])
         nc.sync.dma_start(gate_own[:], gate_rows[:, :OWN])
         for j in range(1, PACK):
             nc.sync.dma_start(x_rows[j][:, :T], x_by_row[j])
-        for start, stop in runs([1024,1024,896], OWN):
+        for start, stop in runs([1280,1792], OWN):
             nc.sync.dma_start(gate_rest[:, start - OWN : stop - OWN], gate_rows[:, start:stop])
         for quad in range(4):
             nc.sync.dma_start(
@@ -88,7 +91,10 @@ def tile_moe_pre_lin_none_kernel(
 
         pieces = runs(PIECES, OWN)
         chunks = runs(SHARED, OWN)
-        raw = {start: keep.tile([P, PACK, stop - start], F32, name=f"raw{start}") for start, stop in chunks}
+        raw = {}
+        for start, stop in chunks:
+            if start != chunks[1][0]:
+                raw[start] = keep.tile([P, PACK, stop - start], F32, name=f"raw{start}")
         helped = {(3072, 0)}
         for start, stop in chunks:
             if (start, 0) in helped:
@@ -96,6 +102,7 @@ def tile_moe_pre_lin_none_kernel(
         products = keep.tile([P, PACK, OWN], F32, name="products")
         for j in range(PACK):
             nc.vector.tensor_tensor(products[:, j, :], picked_x(j, 0, OWN), gate_own[:], MULT)
+        raw[chunks[1][0]] = keep.tile([P, PACK, SHARED[1]], F32, name="raw_second", tag="second")
         for start, stop in chunks:
             if (start, 3) in helped:
                 nc.vector.tensor_copy(raw[start][:, 3, :], picked_x(3, start, stop))
@@ -157,18 +164,32 @@ def tile_moe_pre_lin_none_kernel(
 
         fetched = [keep.tile([P, T], F32, name=f"fetched{r}") for r in range(3)]
         totals = [keep.tile([P, T], F32, name=f"total{r}") for r in range(TOP)]
-        lead, mid, last = slice(0, 256), slice(256, 768), slice(768, T)
-        front = slice(0, last.start)
-        for r, tokens in ((0, mid), (0, last), (1, front), (0, lead), (1, last), (2, last)):
+        lead, mid, late, last = slice(0, 256), slice(256, 512), slice(512, 768), slice(768, T)
+        both = slice(0, 512)
+
+        def fetch(r, tokens):
             nc.scalar.activation(fetched[r][:, tokens], picked(r, tokens), COPY)
+
+        def add_picked(to, r, tokens, onto):
+            nc.vector.tensor_tensor(totals[to][:, tokens], picked(r, tokens), onto[:, tokens], ADD)
+
+        def add_fetched(to, r, tokens):
+            nc.vector.tensor_tensor(totals[to][:, tokens], totals[to - 1][:, tokens], fetched[r][:, tokens], ADD)
+
+        for r, tokens in ((0, mid), (0, slice(512, T)), (0, lead), (1, both), (1, slice(512, T)), (2, last)):
+            fetch(r, tokens)
         nc.vector.tensor_copy(totals[0][:, lead], picked(2, lead))
-        nc.vector.tensor_tensor(totals[1][:, lead], picked(3, lead), totals[0][:, lead], ADD)
-        nc.vector.tensor_tensor(totals[0][:, mid], picked(2, mid), fetched[0][:, mid], ADD)
-        nc.vector.tensor_tensor(totals[1][:, last], picked(3, last), fetched[0][:, last], ADD)
-        nc.vector.tensor_tensor(totals[2][:, mid], picked(3, mid), totals[0][:, mid], ADD)
-        nc.vector.tensor_tensor(totals[2][:, lead], totals[1][:, lead], fetched[0][:, lead], ADD)
-        nc.vector.tensor_tensor(totals[2][:, last], totals[1][:, last], fetched[1][:, last], ADD)
-        nc.vector.tensor_tensor(totals[3][:, front], totals[2][:, front], fetched[1][:, front], ADD)
-        nc.sync.dma_start(out[:, front], totals[3][:, front])
-        nc.vector.tensor_tensor(totals[3][:, last], totals[2][:, last], fetched[2][:, last], ADD)
-        nc.scalar.dma_start(out[:, last], totals[3][:, last])
+        add_picked(1, 2, mid, fetched[0])
+        add_picked(1, 3, lead, totals[0])
+        add_picked(0, 2, late, fetched[0])
+        add_picked(2, 3, mid, totals[1])
+        add_fetched(2, 0, lead)
+        add_picked(1, 3, last, fetched[0])
+        add_fetched(3, 1, both)
+        nc.sync.dma_start(out[:, both], totals[3][:, both])
+        add_picked(2, 3, late, totals[0])
+        add_fetched(2, 1, last)
+        add_fetched(3, 1, late)
+        nc.scalar.dma_start(out[:, late], totals[3][:, late])
+        add_fetched(3, 2, last)
+        nc.sync.dma_start(out[:, last], totals[3][:, last])

@@ -1,6 +1,7 @@
 from contextlib import ExitStack
 
 import concourse.mybir as mybir
+from concourse.masks import make_identity
 
 K, T, E, C, N = 512, 1024, 16, 256, 128
 TOP = 4
@@ -23,9 +24,9 @@ MULT = mybir.AluOpType.mult
 ADD = mybir.AluOpType.add
 COPY = mybir.ActivationFunctionType.Copy
 
-OWN = 1024
-SHARED = [1280,768,512,256,256]
-PIECES = [1280,768,512,256,128,128]
+OWN = 1280
+SHARED = [1280,512,512,256,256]
+PIECES = [512,512,256,512,512,256,128,128]
 UNITS = [1024,1024,1024,512,256,128,128]
 WINDOW = max([OWN] + SHARED) + 32
 NEAR = 2
@@ -46,42 +47,51 @@ def tile_moe_pre_lin_none_kernel(
     nc = tc.nc
     with ExitStack() as ctx:
         keep = ctx.enter_context(tc.tile_pool(name="keep", bufs=1))
-        psum = ctx.enter_context(tc.psum_pool(name="psum", bufs=8))
+        gate_psum = ctx.enter_context(tc.psum_pool(name="gate_psum", bufs=2))
+        psum = ctx.enter_context(tc.psum_pool(name="psum", bufs=6))
 
         slot_list = keep.tile([P, SLOTS // PER_COLUMN], U16, name="slot_list")
         pos_lists = [keep.tile([P, T // PER_COLUMN], U16, name=f"pos_list{r}") for r in range(TOP)]
         x_rows = [keep.tile([P, WINDOW], F32, name=f"x_rows{j}") for j in range(PACK)]
         gate_own = keep.tile([P, OWN], F32, name="gate_own", tag="second")
-        gate_rest = keep.tile([P, SLOTS - OWN], F32, name="gate_rest")
+        gate_blocks = keep.tile([P, P], F32, name="gate_blocks")
+        gate_columns = keep.tile([P, SLOTS // P], F32, name="gate_columns")
+        identity = keep.tile([P, P], F32, name="identity")
         w_codes = keep.tile([P, E, N * PACK], U8, name="w_codes", align_bytes=64)
         w_scale_rows = keep.tile([P, E, N], U8, name="w_scale_rows", align_bytes=64)
         woven = keep.tile([P, SLOTS * PACK], BF16, name="woven", align_bytes=64)
         y = keep.tile([P, SLOTS], F32, name="y")
-
-        x_by_row = xT.rearrange("(p j) t -> j p t", j=PACK)
-        gate_rows = gate.rearrange("(p j) s -> j p s", j=PACK)[0]
-        words_hbm = w_words.rearrange("e a p n r -> p (e a) (n r)").bitcast(I32)
-        scales_hbm = w_scales.rearrange("e a q n -> q (e a) n").bitcast(I32)
-
         warm = keep.tile([P, 2], F32, name="warm")
         nc.gpsimd.memset(warm[:, 0:1], 0.0)
         nc.scalar.activation(warm[:, 1:2], warm[:, 0:1], COPY)
+        make_identity(nc, identity[:])
+
+        x_by_row = xT.rearrange("(p j) t -> j p t", j=PACK)
+        gate_rows = gate.rearrange("(p j) s -> j p s", j=PACK)[0]
+        blocks_hbm = gate.rearrange("k (b c) -> (k b) c", c=P)[:P, :]
+        words_hbm = w_words.rearrange("e a p n r -> p (e a) (n r)").bitcast(I32)
+        scales_hbm = w_scales.rearrange("e a q n -> q (e a) n").bitcast(I32)
+
         nc.vector.memset(w_scale_rows[:].bitcast(I32), 0)
+        nc.sync.dma_start(gate_blocks[:], blocks_hbm)
         nc.sync.dma_start(slot_list[:], offs)
         nc.sync.dma_start(x_rows[0][:, :T], x_by_row[0])
         nc.sync.dma_start(gate_own[:], gate_rows[:, :OWN])
         for j in range(1, PACK):
             nc.sync.dma_start(x_rows[j][:, :T], x_by_row[j])
-        for start, stop in runs([1280,1792], OWN):
-            nc.sync.dma_start(gate_rest[:, start - OWN : stop - OWN], gate_rows[:, start:stop])
         for quad in range(4):
             nc.sync.dma_start(
                 w_scale_rows[32 * quad : 32 * quad + 4, :, :].bitcast(I32), scales_hbm[4 * quad : 4 * quad + 4]
             )
-        for experts in (slice(0, E // 2), slice(E // 2, E)):
+        for e0 in range(0, E, E // 2):
+            experts = slice(e0, e0 + E // 2)
             nc.sync.dma_start(w_codes[:, experts, :].bitcast(I32), words_hbm[:, experts, :])
         for tile, pos in zip(pos_lists, (pos1, pos2, pos3, pos4)):
             nc.sync.dma_start(tile[:], pos)
+
+        turned_gate = gate_psum.tile([P, BANK], F32, name="gate_bank")
+        nc.tensor.transpose(turned_gate[:, :P], gate_blocks[:], identity[:])
+        nc.scalar.copy(out=gate_columns[:], in_=turned_gate[:, : SLOTS // P])
 
         def picked_x(j, start, stop):
             return x_rows[j][:].indirect(slot_list[:, start // PER_COLUMN : stop // PER_COLUMN])
@@ -92,38 +102,48 @@ def tile_moe_pre_lin_none_kernel(
         pieces = runs(PIECES, OWN)
         chunks = runs(SHARED, OWN)
         raw = {}
-        for start, stop in chunks:
-            if start != chunks[1][0]:
-                raw[start] = keep.tile([P, PACK, stop - start], F32, name=f"raw{start}")
-        helped = {(3072, 0)}
-        for start, stop in chunks:
-            if (start, 0) in helped:
-                nc.vector.tensor_copy(raw[start][:, 0, :], picked_x(0, start, stop))
+        for start, stop in chunks[:1] + chunks[2:]:
+            raw[start] = keep.tile([P, PACK, stop - start], F32, name=f"raw{start}")
+        helped = 3072
+        nc.vector.tensor_copy(raw[helped][:, 0, :], picked_x(0, helped, helped + raw[helped].shape[2]))
         products = keep.tile([P, PACK, OWN], F32, name="products")
         for j in range(PACK):
             nc.vector.tensor_tensor(products[:, j, :], picked_x(j, 0, OWN), gate_own[:], MULT)
         raw[chunks[1][0]] = keep.tile([P, PACK, SHARED[1]], F32, name="raw_second", tag="second")
         for start, stop in chunks:
-            if (start, 3) in helped:
-                nc.vector.tensor_copy(raw[start][:, 3, :], picked_x(3, start, stop))
-        for start, stop in chunks:
             for j in range(PACK):
-                if (start, j) not in helped:
+                if (start, j) != (helped, 0):
                     nc.scalar.activation(raw[start][:, j, :], picked_x(j, start, stop), COPY)
-        nc.vector.tensor_copy(woven_view(0, OWN), products[:].rearrange("p j (c i) -> p c j i", i=NEAR))
+        nc.gpsimd.tensor_scalar(
+            woven[:, : PACK * OWN].rearrange("p (c j) -> p c j", j=PACK),
+            products[:].rearrange("p j c -> p c j"),
+            1.0,
+            0.0,
+            MULT,
+            ADD,
+        )
+
+        gate_banks = {}
+
+        def spread_gate(start, stop):
+            bank = gate_psum.tile([P, BANK], F32, name="gate_bank")
+            for c0 in range(0, stop - start, P):
+                block = (start + c0) // P
+                column = gate_columns[:, block : block + 1].to_broadcast([P, P])
+                nc.tensor.transpose(bank[:, c0 : c0 + P], column, identity[:])
+            gate_banks[start] = bank
 
         def times_gate_and_weave(start, stop):
             base = max(s for s in raw if s <= start)
-            n = stop - start
-            gate_view = gate_rest[:, start - OWN : stop - OWN].rearrange("p (c i) -> p c i", i=NEAR)
+            spread_gate(start, stop)
+            first = max(gate_banks)
+            gate_view = gate_banks[first][:, start - first : stop - first].rearrange("p (c i) -> p c i", i=NEAR)
             nc.vector.tensor_tensor(
                 woven_view(start, stop),
                 raw[base][:, :, start - base : stop - base].rearrange("p j (c i) -> p c j i", i=NEAR),
-                gate_view.unsqueeze(2).to_broadcast([P, n // NEAR, PACK, NEAR]),
+                gate_view.unsqueeze(2).to_broadcast([P, (stop - start) // NEAR, PACK, NEAR]),
                 MULT,
             )
-
-        filled = []
 
         def quantise_and_multiply(start, stop):
             n = stop - start

@@ -24,11 +24,12 @@ MULT = mybir.AluOpType.mult
 ADD = mybir.AluOpType.add
 COPY = mybir.ActivationFunctionType.Copy
 
-OWN = 1280
-SHARED = [1280,512,512,256,256]
-PIECES = [512,512,256,512,512,256,128,128]
+OWN = 1024
+SHARED = [1024,512,512,512,256,256]
+PIECES = [512,512,512,512,512,256,128,128]
 UNITS = [1024,1024,1024,512,256,128,128]
 WINDOW = max([OWN] + SHARED) + 32
+HELP = 512
 NEAR = 2
 
 
@@ -47,19 +48,20 @@ def tile_moe_pre_lin_none_kernel(
     nc = tc.nc
     with ExitStack() as ctx:
         keep = ctx.enter_context(tc.tile_pool(name="keep", bufs=1))
+        reuse = ctx.enter_context(tc.tile_pool(name="reuse", bufs=1))
         gate_psum = ctx.enter_context(tc.psum_pool(name="gate_psum", bufs=2))
         psum = ctx.enter_context(tc.psum_pool(name="psum", bufs=6))
 
         slot_list = keep.tile([P, SLOTS // PER_COLUMN], U16, name="slot_list")
         pos_lists = [keep.tile([P, T // PER_COLUMN], U16, name=f"pos_list{r}") for r in range(TOP)]
         x_rows = [keep.tile([P, WINDOW], F32, name=f"x_rows{j}") for j in range(PACK)]
-        gate_own = keep.tile([P, OWN], F32, name="gate_own", tag="second")
+        gate_own = keep.tile([P, OWN], F32, name="gate_own", tag="gate_own")
+        gate_second = keep.tile([P, SHARED[1]], F32, name="gate_second")
         gate_blocks = keep.tile([P, P], F32, name="gate_blocks")
         gate_columns = keep.tile([P, SLOTS // P], F32, name="gate_columns")
         identity = keep.tile([P, P], F32, name="identity")
         w_codes = keep.tile([P, E, N * PACK], U8, name="w_codes", align_bytes=64)
         w_scale_rows = keep.tile([P, E, N], U8, name="w_scale_rows", align_bytes=64)
-        woven = keep.tile([P, SLOTS * PACK], BF16, name="woven", align_bytes=64)
         y = keep.tile([P, SLOTS], F32, name="y")
         warm = keep.tile([P, 2], F32, name="warm")
         nc.gpsimd.memset(warm[:, 0:1], 0.0)
@@ -76,9 +78,11 @@ def tile_moe_pre_lin_none_kernel(
         nc.sync.dma_start(gate_blocks[:], blocks_hbm)
         nc.sync.dma_start(slot_list[:], offs)
         nc.sync.dma_start(x_rows[0][:, :T], x_by_row[0])
-        nc.sync.dma_start(gate_own[:], gate_rows[:, :OWN])
-        for j in range(1, PACK):
+        for j in range(1, PACK - 1):
             nc.sync.dma_start(x_rows[j][:, :T], x_by_row[j])
+        nc.sync.dma_start(gate_own[:], gate_rows[:, :OWN])
+        nc.sync.dma_start(x_rows[PACK - 1][:, :T], x_by_row[PACK - 1])
+        nc.sync.dma_start(gate_second[:], gate_rows[:, OWN + SHARED[0] : OWN + SHARED[0] + SHARED[1]])
         for quad in range(4):
             nc.sync.dma_start(
                 w_scale_rows[32 * quad : 32 * quad + 4, :, :].bitcast(I32), scales_hbm[4 * quad : 4 * quad + 4]
@@ -96,32 +100,55 @@ def tile_moe_pre_lin_none_kernel(
         def picked_x(j, start, stop):
             return x_rows[j][:].indirect(slot_list[:, start // PER_COLUMN : stop // PER_COLUMN])
 
-        def woven_view(start, stop):
-            return woven[:, PACK * start : PACK * stop].rearrange("p (c i j) -> p c j i", i=NEAR, j=PACK)
-
-        pieces = runs(PIECES, OWN)
         chunks = runs(SHARED, OWN)
-        raw = {}
-        for start, stop in chunks[:1] + chunks[2:]:
-            raw[start] = keep.tile([P, PACK, stop - start], F32, name=f"raw{start}")
-        helped = 3072
-        nc.vector.tensor_copy(raw[helped][:, 0, :], picked_x(0, helped, helped + raw[helped].shape[2]))
-        products = keep.tile([P, PACK, OWN], F32, name="products")
+        units = runs(UNITS)
+        raw = {start: keep.tile([P, PACK, stop - start], F32, name=f"raw{start}") for start, stop in chunks[:3]}
+        first, second = chunks[0], chunks[1]
+        split = first[0] + HELP
+        for j in range(PACK - 1):
+            nc.vector.tensor_copy(raw[first[0]][:, j, :HELP], picked_x(j, first[0], split))
+        products = reuse.tile([P, PACK, OWN], F32, name="products", offset=0)
         for j in range(PACK):
             nc.vector.tensor_tensor(products[:, j, :], picked_x(j, 0, OWN), gate_own[:], MULT)
-        raw[chunks[1][0]] = keep.tile([P, PACK, SHARED[1]], F32, name="raw_second", tag="second")
-        for start, stop in chunks:
+        raw[chunks[3][0]] = keep.tile([P, PACK, SHARED[3]], F32, name="raw_fourth", tag="gate_own")
+
+        def fetch_chunk(start, stop):
             for j in range(PACK):
-                if (start, j) != (helped, 0):
-                    nc.scalar.activation(raw[start][:, j, :], picked_x(j, start, stop), COPY)
+                begin = split if start == first[0] and j < PACK - 1 else start
+                nc.scalar.activation(raw[start][:, j, begin - start :], picked_x(j, begin, stop), COPY)
+
+        for chunk in chunks[:4]:
+            fetch_chunk(*chunk)
+
+        woven = {}
+
+        def new_woven(unit, tag):
+            start, stop = units[unit]
+            woven[start] = keep.tile([P, PACK * (stop - start)], BF16, name=f"woven{start}", tag=tag, align_bytes=64)
+
+        def woven_run(start, stop):
+            base = max(s for s in woven if s <= start)
+            return woven[base][:, PACK * (start - base) : PACK * (stop - base)]
+
+        def woven_view(start, stop):
+            return woven_run(start, stop).rearrange("p (c i j) -> p c j i", i=NEAR, j=PACK)
+
+        for unit in range(len(units)):
+            if unit != 2:
+                new_woven(unit, f"woven{unit}")
         nc.gpsimd.tensor_scalar(
-            woven[:, : PACK * OWN].rearrange("p (c j) -> p c j", j=PACK),
+            woven_run(0, OWN).rearrange("p (c j) -> p c j", j=PACK),
             products[:].rearrange("p j c -> p c j"),
             1.0,
             0.0,
             MULT,
             ADD,
         )
+
+        for start, stop in chunks[4:]:
+            place = 4 * PACK * (start - chunks[4][0])
+            raw[start] = reuse.tile([P, PACK, stop - start], F32, name=f"raw{start}", offset=place)
+            fetch_chunk(start, stop)
 
         gate_banks = {}
 
@@ -150,7 +177,7 @@ def tile_moe_pre_lin_none_kernel(
             codes = keep.tile([P, n], U32, name=f"codes{start}", align_bytes=64)
             scale_rows = keep.tile([P, n], U8, name=f"scale_rows{start}", align_bytes=64)
             nc.vector.quantize_mx(
-                out=codes[:].bitcast(FP8X4), scales=scale_rows[:], in_=woven[:, PACK * start : PACK * stop]
+                out=codes[:].bitcast(FP8X4), scales=scale_rows[:], in_=woven_run(start, stop)
             )
             for b0 in range(0, n, BANK):
                 acc = psum.tile([P, BANK], F32, name="acc")
@@ -169,15 +196,26 @@ def tile_moe_pre_lin_none_kernel(
                     )
                 nc.scalar.copy(out=y[:, start + b0 : start + b0 + width], in_=acc[:, :width])
 
-        done = 0
-        units = runs(UNITS)
-        for start, stop in pieces + [(SLOTS, SLOTS)]:
-            if start < SLOTS:
-                times_gate_and_weave(start, stop)
-            for u0, u1 in units:
-                if done <= u0 and u1 <= start:
-                    quantise_and_multiply(u0, u1)
-                    done = u1
+        pieces = [piece for piece in runs(PIECES, OWN) if piece != second]
+        for piece in pieces[:2]:
+            times_gate_and_weave(*piece)
+        quantise_and_multiply(*units[1])
+        quantise_and_multiply(*units[0])
+        new_woven(2, "woven0")
+        nc.gpsimd.tensor_tensor(
+            woven_run(*second).rearrange("p (c j) -> p c j", j=PACK),
+            raw[second[0]][:].rearrange("p j c -> p c j"),
+            gate_second[:].unsqueeze(2).to_broadcast([P, SHARED[1], PACK]),
+            MULT,
+        )
+        for piece in pieces[2:5]:
+            times_gate_and_weave(*piece)
+        quantise_and_multiply(*units[2])
+        times_gate_and_weave(*pieces[5])
+        quantise_and_multiply(*units[3])
+        times_gate_and_weave(*pieces[6])
+        for unit in units[4:]:
+            quantise_and_multiply(*unit)
 
         def picked(r, tokens):
             return y[:].indirect(pos_lists[r][:, tokens.start // PER_COLUMN : tokens.stop // PER_COLUMN])

@@ -25,9 +25,9 @@ ADD = mybir.AluOpType.add
 COPY = mybir.ActivationFunctionType.Copy
 
 OWN = 1024
-SHARED = [1024,512,512,512,256,256]
-PIECES = [512,512,512,512,512,256,128,128]
-UNITS = [1024,1024,1024,512,256,128,128]
+SHARED = [1280,512,512,384,256,128]
+PIECES = [512,512,256,512,512,384,256,128]
+UNITS = [1024,1024,256,1024,512,128,128]
 WINDOW = max([OWN] + SHARED) + 32
 HELP = 512
 NEAR = 2
@@ -55,7 +55,11 @@ def tile_moe_pre_lin_none_kernel(
         slot_list = keep.tile([P, SLOTS // PER_COLUMN], U16, name="slot_list")
         pos_lists = [keep.tile([P, T // PER_COLUMN], U16, name=f"pos_list{r}") for r in range(TOP)]
         x_rows = [keep.tile([P, WINDOW], F32, name=f"x_rows{j}") for j in range(PACK)]
-        gate_own = keep.tile([P, OWN], F32, name="gate_own", tag="gate_own")
+        half = OWN // 2
+        gate_own = [
+            reuse.tile([P, half], F32, name="gate_low", offset=4 * PACK * (OWN + SHARED[1]) - 2 * half),
+            keep.tile([P, half], F32, name="gate_high", tag="gate_high"),
+        ]
         gate_second = keep.tile([P, SHARED[1]], F32, name="gate_second")
         gate_blocks = keep.tile([P, P], F32, name="gate_blocks")
         gate_columns = keep.tile([P, SLOTS // P], F32, name="gate_columns")
@@ -75,13 +79,14 @@ def tile_moe_pre_lin_none_kernel(
         scales_hbm = w_scales.rearrange("e a q n -> q (e a) n").bitcast(I32)
 
         nc.vector.memset(w_scale_rows[:].bitcast(I32), 0)
-        nc.sync.dma_start(gate_blocks[:], blocks_hbm)
         nc.sync.dma_start(slot_list[:], offs)
         nc.sync.dma_start(x_rows[0][:, :T], x_by_row[0])
         for j in range(1, PACK - 1):
             nc.sync.dma_start(x_rows[j][:, :T], x_by_row[j])
-        nc.sync.dma_start(gate_own[:], gate_rows[:, :OWN])
+        nc.sync.dma_start(gate_own[0][:], gate_rows[:, :half])
         nc.sync.dma_start(x_rows[PACK - 1][:, :T], x_by_row[PACK - 1])
+        nc.sync.dma_start(gate_own[1][:], gate_rows[:, half:OWN])
+        nc.sync.dma_start(gate_blocks[:], blocks_hbm)
         nc.sync.dma_start(gate_second[:], gate_rows[:, OWN + SHARED[0] : OWN + SHARED[0] + SHARED[1]])
         for quad in range(4):
             nc.sync.dma_start(
@@ -102,15 +107,20 @@ def tile_moe_pre_lin_none_kernel(
 
         chunks = runs(SHARED, OWN)
         units = runs(UNITS)
-        raw = {start: keep.tile([P, PACK, stop - start], F32, name=f"raw{start}") for start, stop in chunks[:3]}
+        raw = {start: keep.tile([P, PACK, stop - start], F32, name=f"raw{start}") for start, stop in chunks[:1]}
         first, second = chunks[0], chunks[1]
         split = first[0] + HELP
         for j in range(PACK - 1):
             nc.vector.tensor_copy(raw[first[0]][:, j, :HELP], picked_x(j, first[0], split))
         products = reuse.tile([P, PACK, OWN], F32, name="products", offset=0)
-        for j in range(PACK):
-            nc.vector.tensor_tensor(products[:, j, :], picked_x(j, 0, OWN), gate_own[:], MULT)
-        raw[chunks[3][0]] = keep.tile([P, PACK, SHARED[3]], F32, name="raw_fourth", tag="gate_own")
+        for h in range(2):
+            for j in range(PACK):
+                cols = slice(h * half, (h + 1) * half)
+                nc.vector.tensor_tensor(products[:, j, cols], picked_x(j, cols.start, cols.stop), gate_own[h][:], MULT)
+        for start, stop in chunks[1:3]:
+            place = 4 * PACK * (OWN + start - second[0])
+            raw[start] = reuse.tile([P, PACK, stop - start], F32, name=f"raw{start}", offset=place)
+        raw[chunks[3][0]] = keep.tile([P, PACK, SHARED[3]], F32, name="raw_fourth", tag="gate_high")
 
         def fetch_chunk(start, stop):
             for j in range(PACK):
@@ -122,8 +132,7 @@ def tile_moe_pre_lin_none_kernel(
 
         woven = {}
 
-        def new_woven(unit, tag):
-            start, stop = units[unit]
+        def new_woven(start, stop, tag):
             woven[start] = keep.tile([P, PACK * (stop - start)], BF16, name=f"woven{start}", tag=tag, align_bytes=64)
 
         def woven_run(start, stop):
@@ -133,9 +142,9 @@ def tile_moe_pre_lin_none_kernel(
         def woven_view(start, stop):
             return woven_run(start, stop).rearrange("p (c i j) -> p c j i", i=NEAR, j=PACK)
 
-        for unit in range(len(units)):
-            if unit != 2:
-                new_woven(unit, f"woven{unit}")
+        new_woven(0, OWN, "woven_first")
+        new_woven(OWN, second[0], "woven_second")
+        new_woven(second[0] + OWN, SLOTS, "woven_last")
         nc.gpsimd.tensor_scalar(
             woven_run(0, OWN).rearrange("p (c j) -> p c j", j=PACK),
             products[:].rearrange("p j c -> p c j"),
@@ -197,21 +206,20 @@ def tile_moe_pre_lin_none_kernel(
                 nc.scalar.copy(out=y[:, start + b0 : start + b0 + width], in_=acc[:, :width])
 
         pieces = [piece for piece in runs(PIECES, OWN) if piece != second]
-        for piece in pieces[:2]:
+        for piece in pieces[:3]:
             times_gate_and_weave(*piece)
         quantise_and_multiply(*units[1])
+        quantise_and_multiply(*units[2])
         quantise_and_multiply(*units[0])
-        new_woven(2, "woven0")
+        new_woven(second[0], second[0] + OWN, "woven_first")
         nc.gpsimd.tensor_tensor(
             woven_run(*second).rearrange("p (c j) -> p c j", j=PACK),
             raw[second[0]][:].rearrange("p j c -> p c j"),
             gate_second[:].unsqueeze(2).to_broadcast([P, SHARED[1], PACK]),
             MULT,
         )
-        for piece in pieces[2:5]:
+        for piece in pieces[3:6]:
             times_gate_and_weave(*piece)
-        quantise_and_multiply(*units[2])
-        times_gate_and_weave(*pieces[5])
         quantise_and_multiply(*units[3])
         times_gate_and_weave(*pieces[6])
         for unit in units[4:]:

@@ -25,21 +25,20 @@ ADD = mybir.AluOpType.add
 COPY = mybir.ActivationFunctionType.Copy
 
 OWN = 1024
-SHARED = [1280,512,512,384,256,128]
-PIECES = [512,512,256,512,512,384,256,128]
-UNITS = [1024,1024,256,1024,512,128,128]
-WINDOW = max([OWN] + SHARED) + 32
+CHUNKS = [1280, 1024, 512, 256]
+POOL_SHARE = 512
 HELP = 512
+WINDOW = max([OWN] + CHUNKS) + 32
 NEAR = 2
 
 
-def starts(widths, first=0):
-    return [first + sum(widths[:i]) for i in range(len(widths) + 1)]
-
-
-def runs(widths, first=0):
-    edges = starts(widths, first)
+def runs(widths, first):
+    edges = [first + sum(widths[:i]) for i in range(len(widths) + 1)]
     return list(zip(edges, edges[1:]))
+
+
+def cut(start, stop, width):
+    return [(s, min(s + width, stop)) for s in range(start, stop, width)]
 
 
 def tile_moe_pre_lin_none_kernel(
@@ -49,19 +48,19 @@ def tile_moe_pre_lin_none_kernel(
     with ExitStack() as ctx:
         keep = ctx.enter_context(tc.tile_pool(name="keep", bufs=1))
         reuse = ctx.enter_context(tc.tile_pool(name="reuse", bufs=1))
-        gate_psum = ctx.enter_context(tc.psum_pool(name="gate_psum", bufs=2))
-        psum = ctx.enter_context(tc.psum_pool(name="psum", bufs=6))
+        gate_psum = ctx.enter_context(tc.psum_pool(name="gate_psum", bufs=3))
+        psum = ctx.enter_context(tc.psum_pool(name="psum", bufs=3))
+
+        chunks = runs(CHUNKS, OWN)
+        first = chunks[0]
+        pool_run = (first[1], first[1] + POOL_SHARE)
 
         slot_list = keep.tile([P, SLOTS // PER_COLUMN], U16, name="slot_list")
         pos_lists = [keep.tile([P, T // PER_COLUMN], U16, name=f"pos_list{r}") for r in range(TOP)]
         x_rows = [keep.tile([P, WINDOW], F32, name=f"x_rows{j}") for j in range(PACK)]
-        half = OWN // 2
-        gate_own = [
-            reuse.tile([P, half], F32, name="gate_low", offset=4 * PACK * (OWN + SHARED[1]) - 2 * half),
-            keep.tile([P, half], F32, name="gate_high", tag="gate_high"),
-        ]
-        gate_second = keep.tile([P, SHARED[1]], F32, name="gate_second")
-        gate_blocks = keep.tile([P, P], F32, name="gate_blocks")
+        gate_own = keep.tile([P, OWN], F32, name="gate_own")
+        gate_pool = keep.tile([P, POOL_SHARE], F32, name="gate_pool")
+        gate_blocks = reuse.tile([P, P], F32, name="gate_blocks", offset=0)
         gate_columns = keep.tile([P, SLOTS // P], F32, name="gate_columns")
         identity = keep.tile([P, P], F32, name="identity")
         w_codes = keep.tile([P, E, N * PACK], U8, name="w_codes", align_bytes=64)
@@ -78,16 +77,14 @@ def tile_moe_pre_lin_none_kernel(
         words_hbm = w_words.rearrange("e a p n r -> p (e a) (n r)").bitcast(I32)
         scales_hbm = w_scales.rearrange("e a q n -> q (e a) n").bitcast(I32)
 
-        nc.vector.memset(w_scale_rows[:].bitcast(I32), 0)
+        nc.gpsimd.memset(w_scale_rows[:].bitcast(I32), 0)
         nc.sync.dma_start(slot_list[:], offs)
-        nc.sync.dma_start(x_rows[0][:, :T], x_by_row[0])
-        for j in range(1, PACK - 1):
+        for j in range(PACK - 1):
             nc.sync.dma_start(x_rows[j][:, :T], x_by_row[j])
-        nc.sync.dma_start(gate_own[0][:], gate_rows[:, :half])
+        nc.sync.dma_start(gate_own[:], gate_rows[:, :OWN])
         nc.sync.dma_start(x_rows[PACK - 1][:, :T], x_by_row[PACK - 1])
-        nc.sync.dma_start(gate_own[1][:], gate_rows[:, half:OWN])
         nc.sync.dma_start(gate_blocks[:], blocks_hbm)
-        nc.sync.dma_start(gate_second[:], gate_rows[:, OWN + SHARED[0] : OWN + SHARED[0] + SHARED[1]])
+        nc.sync.dma_start(gate_pool[:], gate_rows[:, pool_run[0] : pool_run[1]])
         for quad in range(4):
             nc.sync.dma_start(
                 w_scale_rows[32 * quad : 32 * quad + 4, :, :].bitcast(I32), scales_hbm[4 * quad : 4 * quad + 4]
@@ -105,30 +102,23 @@ def tile_moe_pre_lin_none_kernel(
         def picked_x(j, start, stop):
             return x_rows[j][:].indirect(slot_list[:, start // PER_COLUMN : stop // PER_COLUMN])
 
-        chunks = runs(SHARED, OWN)
-        units = runs(UNITS)
-        raw = {start: keep.tile([P, PACK, stop - start], F32, name=f"raw{start}") for start, stop in chunks[:1]}
-        first, second = chunks[0], chunks[1]
+        raw_first = keep.tile([P, PACK, CHUNKS[0]], F32, name="raw_first")
+        raw_later = reuse.tile([P, PACK * (SLOTS - first[1])], F32, name="raw_later", offset=0)
+        raw = {first[0]: raw_first[:]}
+        for start, stop in chunks[1:]:
+            run = raw_later[:, PACK * (start - first[1]) : PACK * (stop - first[1])]
+            raw[start] = run.rearrange("p (j c) -> p j c", j=PACK)
+
         split = first[0] + HELP
         for j in range(PACK - 1):
             nc.vector.tensor_copy(raw[first[0]][:, j, :HELP], picked_x(j, first[0], split))
-        products = reuse.tile([P, PACK, OWN], F32, name="products", offset=0)
-        for h in range(2):
-            for j in range(PACK):
-                cols = slice(h * half, (h + 1) * half)
-                nc.vector.tensor_tensor(products[:, j, cols], picked_x(j, cols.start, cols.stop), gate_own[h][:], MULT)
-        for start, stop in chunks[1:3]:
-            place = 4 * PACK * (OWN + start - second[0])
-            raw[start] = reuse.tile([P, PACK, stop - start], F32, name=f"raw{start}", offset=place)
-        raw[chunks[3][0]] = keep.tile([P, PACK, SHARED[3]], F32, name="raw_fourth", tag="gate_high")
-
-        def fetch_chunk(start, stop):
+        products = keep.tile([P, PACK, OWN], F32, name="products")
+        for j in range(PACK):
+            nc.vector.tensor_tensor(products[:, j, :], picked_x(j, 0, OWN), gate_own[:], MULT)
+        for start, stop in chunks:
             for j in range(PACK):
                 begin = split if start == first[0] and j < PACK - 1 else start
                 nc.scalar.activation(raw[start][:, j, begin - start :], picked_x(j, begin, stop), COPY)
-
-        for chunk in chunks[:4]:
-            fetch_chunk(*chunk)
 
         woven = {}
 
@@ -139,12 +129,9 @@ def tile_moe_pre_lin_none_kernel(
             base = max(s for s in woven if s <= start)
             return woven[base][:, PACK * (start - base) : PACK * (stop - base)]
 
-        def woven_view(start, stop):
-            return woven_run(start, stop).rearrange("p (c i j) -> p c j i", i=NEAR, j=PACK)
-
-        new_woven(0, OWN, "woven_first")
-        new_woven(OWN, second[0], "woven_second")
-        new_woven(second[0] + OWN, SLOTS, "woven_last")
+        new_woven(0, OWN, "woven_pool")
+        new_woven(OWN, first[1], "woven_first")
+        new_woven(pool_run[1], SLOTS, "woven_last")
         nc.gpsimd.tensor_scalar(
             woven_run(0, OWN).rearrange("p (c j) -> p c j", j=PACK),
             products[:].rearrange("p j c -> p c j"),
@@ -154,76 +141,69 @@ def tile_moe_pre_lin_none_kernel(
             ADD,
         )
 
-        for start, stop in chunks[4:]:
-            place = 4 * PACK * (start - chunks[4][0])
-            raw[start] = reuse.tile([P, PACK, stop - start], F32, name=f"raw{start}", offset=place)
-            fetch_chunk(start, stop)
-
-        gate_banks = {}
-
-        def spread_gate(start, stop):
+        def times_gate_and_weave(start, stop):
             bank = gate_psum.tile([P, BANK], F32, name="gate_bank")
             for c0 in range(0, stop - start, P):
                 block = (start + c0) // P
                 column = gate_columns[:, block : block + 1].to_broadcast([P, P])
                 nc.tensor.transpose(bank[:, c0 : c0 + P], column, identity[:])
-            gate_banks[start] = bank
-
-        def times_gate_and_weave(start, stop):
             base = max(s for s in raw if s <= start)
-            spread_gate(start, stop)
-            first = max(gate_banks)
-            gate_view = gate_banks[first][:, start - first : stop - first].rearrange("p (c i) -> p c i", i=NEAR)
+            gate_view = bank[:, : stop - start].rearrange("p (c i) -> p c i", i=NEAR)
             nc.vector.tensor_tensor(
-                woven_view(start, stop),
+                woven_run(start, stop).rearrange("p (c i j) -> p c j i", i=NEAR, j=PACK),
                 raw[base][:, :, start - base : stop - base].rearrange("p j (c i) -> p c j i", i=NEAR),
                 gate_view.unsqueeze(2).to_broadcast([P, (stop - start) // NEAR, PACK, NEAR]),
                 MULT,
             )
 
-        def quantise_and_multiply(start, stop):
-            n = stop - start
-            codes = keep.tile([P, n], U32, name=f"codes{start}", align_bytes=64)
-            scale_rows = keep.tile([P, n], U8, name=f"scale_rows{start}", align_bytes=64)
-            nc.vector.quantize_mx(
-                out=codes[:].bitcast(FP8X4), scales=scale_rows[:], in_=woven_run(start, stop)
-            )
-            for b0 in range(0, n, BANK):
-                acc = psum.tile([P, BANK], F32, name="acc")
-                width = min(n, BANK)
-                for c0 in range(b0, b0 + width, C):
-                    cols = slice(c0, min(c0 + C, n))
-                    expert = (start + c0) // C
-                    nc.tensor.matmul_mx(
-                        out=acc[:, cols.start - b0 : cols.stop - b0],
-                        lhsT=w_codes[:, expert, :].bitcast(FP8X4),
-                        lhsT_scale=w_scale_rows[:, expert, :],
-                        rhs=codes[:, cols].bitcast(FP8X4),
-                        rhs_scale=scale_rows[:, cols],
-                        start=True,
-                        stop=True,
-                    )
-                nc.scalar.copy(out=y[:, start + b0 : start + b0 + width], in_=acc[:, :width])
+        def quantise(start, stop):
+            codes = keep.tile([P, stop - start], U32, name=f"codes{start}", align_bytes=64)
+            scale_rows = keep.tile([P, stop - start], U8, name=f"scale_rows{start}", align_bytes=64)
+            nc.vector.quantize_mx(out=codes[:].bitcast(FP8X4), scales=scale_rows[:], in_=woven_run(start, stop))
+            return start, codes, scale_rows
 
-        pieces = [piece for piece in runs(PIECES, OWN) if piece != second]
-        for piece in pieces[:3]:
+        def multiply(unit, start, stop, empty, banks=psum, tag="acc"):
+            base, codes, scale_rows = unit
+            acc = banks.tile([P, BANK], F32, name=tag)
+            for s0, s1 in cut(start, stop, C):
+                nc.tensor.matmul_mx(
+                    out=acc[:, s0 - start : s1 - start],
+                    lhsT=w_codes[:, s0 // C, :].bitcast(FP8X4),
+                    lhsT_scale=w_scale_rows[:, s0 // C, :],
+                    rhs=codes[:, s0 - base : s1 - base].bitcast(FP8X4),
+                    rhs_scale=scale_rows[:, s0 - base : s1 - base],
+                    start=True,
+                    stop=True,
+                )
+            empty(out=y[:, start:stop], in_=acc[:, : stop - start])
+
+        def quantise_and_multiply(start, stop):
+            unit = quantise(start, stop)
+            for s0, s1 in cut(start, stop, BANK):
+                multiply(unit, s0, s1, nc.scalar.copy)
+
+        for piece in cut(*first, BANK):
             times_gate_and_weave(*piece)
-        quantise_and_multiply(*units[1])
-        quantise_and_multiply(*units[2])
-        quantise_and_multiply(*units[0])
-        new_woven(second[0], second[0] + OWN, "woven_first")
+        for unit in cut(*first, 2 * BANK) + [(0, OWN)]:
+            quantise_and_multiply(*unit)
+        new_woven(*pool_run, "woven_pool")
         nc.gpsimd.tensor_tensor(
-            woven_run(*second).rearrange("p (c j) -> p c j", j=PACK),
-            raw[second[0]][:].rearrange("p j c -> p c j"),
-            gate_second[:].unsqueeze(2).to_broadcast([P, SHARED[1], PACK]),
+            woven_run(*pool_run).rearrange("p (c j) -> p c j", j=PACK),
+            raw[pool_run[0]][:, :, :POOL_SHARE].rearrange("p j c -> p c j"),
+            gate_pool[:].unsqueeze(2).to_broadcast([P, POOL_SHARE, PACK]),
             MULT,
         )
-        for piece in pieces[3:6]:
+        late = cut(pool_run[1], SLOTS, BANK)
+        for piece in late:
             times_gate_and_weave(*piece)
-        quantise_and_multiply(*units[3])
-        times_gate_and_weave(*pieces[6])
-        for unit in units[4:]:
+        for unit in late[:-1]:
             quantise_and_multiply(*unit)
+        pool_unit = quantise(*pool_run)
+        last_unit = quantise(*late[-1])
+        multiply(pool_unit, pool_run[0], pool_run[0] + C, nc.vector.tensor_copy)
+        multiply(pool_unit, pool_run[0] + C, pool_run[1], nc.scalar.copy, gate_psum, "gate_bank")
+        for piece in cut(*late[-1], P):
+            multiply(last_unit, *piece, nc.vector.tensor_copy, gate_psum, "gate_bank")
 
         def picked(r, tokens):
             return y[:].indirect(pos_lists[r][:, tokens.start // PER_COLUMN : tokens.stop // PER_COLUMN])

@@ -24,11 +24,13 @@ MULT = mybir.AluOpType.mult
 ADD = mybir.AluOpType.add
 COPY = mybir.ActivationFunctionType.Copy
 
-OWN = 1024
-CHUNKS = [1280, 1024, 512, 256]
-POOL_SHARE = 512
-HELP = 512
-WINDOW = max([OWN] + CHUNKS) + 32
+OWN = 512
+POOL_FIRST = 896
+COPIED = 896
+LATE_CHUNKS = [1024, 512, 256]
+POOL_SECOND = 512
+HELP = 192
+WINDOW = T + 32
 NEAR = 2
 
 
@@ -47,20 +49,20 @@ def tile_moe_pre_lin_none_kernel(
     nc = tc.nc
     with ExitStack() as ctx:
         keep = ctx.enter_context(tc.tile_pool(name="keep", bufs=1))
-        reuse = ctx.enter_context(tc.tile_pool(name="reuse", bufs=1))
+        after_blocks = ctx.enter_context(tc.tile_pool(name="after_blocks", bufs=1))
         gate_psum = ctx.enter_context(tc.psum_pool(name="gate_psum", bufs=3))
         psum = ctx.enter_context(tc.psum_pool(name="psum", bufs=3))
 
-        chunks = runs(CHUNKS, OWN)
-        first = chunks[0]
-        pool_run = (first[1], first[1] + POOL_SHARE)
+        own, pool_first, copied = runs([OWN, POOL_FIRST, COPIED], 0)
+        late_chunks = runs(LATE_CHUNKS, copied[1])
+        pool_second = (copied[1], copied[1] + POOL_SECOND)
 
         slot_list = keep.tile([P, SLOTS // PER_COLUMN], U16, name="slot_list")
         pos_lists = [keep.tile([P, T // PER_COLUMN], U16, name=f"pos_list{r}") for r in range(TOP)]
         x_rows = [keep.tile([P, WINDOW], F32, name=f"x_rows{j}") for j in range(PACK)]
         gate_own = keep.tile([P, OWN], F32, name="gate_own")
-        gate_pool = keep.tile([P, POOL_SHARE], F32, name="gate_pool")
-        gate_blocks = reuse.tile([P, P], F32, name="gate_blocks", offset=0)
+        gate_pool = {run: keep.tile([P, run[1] - run[0]], F32, name=f"gate{run[0]}") for run in (pool_first, pool_second)}
+        gate_blocks = after_blocks.tile([P, P], F32, name="gate_blocks", offset=4 * (PACK * COPIED - P // 2))
         gate_columns = keep.tile([P, SLOTS // P], F32, name="gate_columns")
         identity = keep.tile([P, P], F32, name="identity")
         w_codes = keep.tile([P, E, N * PACK], U8, name="w_codes", align_bytes=64)
@@ -79,12 +81,13 @@ def tile_moe_pre_lin_none_kernel(
 
         nc.gpsimd.memset(w_scale_rows[:].bitcast(I32), 0)
         nc.sync.dma_start(slot_list[:], offs)
-        for j in range(PACK - 1):
-            nc.sync.dma_start(x_rows[j][:, :T], x_by_row[j])
+        nc.sync.dma_start(x_rows[0][:, :T], x_by_row[0])
         nc.sync.dma_start(gate_own[:], gate_rows[:, :OWN])
-        nc.sync.dma_start(x_rows[PACK - 1][:, :T], x_by_row[PACK - 1])
+        for j in range(1, PACK):
+            nc.sync.dma_start(x_rows[j][:, :T], x_by_row[j])
         nc.sync.dma_start(gate_blocks[:], blocks_hbm)
-        nc.sync.dma_start(gate_pool[:], gate_rows[:, pool_run[0] : pool_run[1]])
+        for run, tile in gate_pool.items():
+            nc.sync.dma_start(tile[:], gate_rows[:, run[0] : run[1]])
         for quad in range(4):
             nc.sync.dma_start(
                 w_scale_rows[32 * quad : 32 * quad + 4, :, :].bitcast(I32), scales_hbm[4 * quad : 4 * quad + 4]
@@ -102,23 +105,29 @@ def tile_moe_pre_lin_none_kernel(
         def picked_x(j, start, stop):
             return x_rows[j][:].indirect(slot_list[:, start // PER_COLUMN : stop // PER_COLUMN])
 
-        raw_first = keep.tile([P, PACK, CHUNKS[0]], F32, name="raw_first")
-        raw_later = reuse.tile([P, PACK * (SLOTS - first[1])], F32, name="raw_later", offset=0)
-        raw = {first[0]: raw_first[:]}
-        for start, stop in chunks[1:]:
-            run = raw_later[:, PACK * (start - first[1]) : PACK * (stop - first[1])]
-            raw[start] = run.rearrange("p (j c) -> p j c", j=PACK)
-
-        split = first[0] + HELP
-        for j in range(PACK - 1):
-            nc.vector.tensor_copy(raw[first[0]][:, j, :HELP], picked_x(j, first[0], split))
+        raw = {}
+        raw_first = keep.tile([P, PACK, POOL_FIRST], F32, name="raw_first", tag="raw_first", align_bytes=64)
+        raw[pool_first[0]] = raw_first[:]
+        nc.vector.tensor_copy(raw_first[:, 0, :HELP], picked_x(0, pool_first[0], pool_first[0] + HELP))
         products = keep.tile([P, PACK, OWN], F32, name="products")
         for j in range(PACK):
-            nc.vector.tensor_tensor(products[:, j, :], picked_x(j, 0, OWN), gate_own[:], MULT)
-        for start, stop in chunks:
+            nc.vector.tensor_tensor(products[:, j, :], picked_x(j, *own), gate_own[:], MULT)
+        raw_copied = after_blocks.tile([P, PACK, COPIED], F32, name="raw_copied", offset=0)
+        raw[copied[0]] = raw_copied[:]
+        for j in range(PACK):
+            nc.vector.tensor_copy(raw_copied[:, j, :], picked_x(j, *copied))
+
+        def fetch_x(base, j, start, stop):
+            nc.scalar.activation(raw[base][:, j, start - base : stop - base], picked_x(j, start, stop), COPY)
+
+        for j in range(PACK):
+            fetch_x(pool_first[0], j, pool_first[0] + (HELP if j == 0 else 0), pool_first[1])
+        raw_late = after_blocks.tile([P, PACK * (SLOTS - copied[1])], F32, name="raw_late", offset=4 * PACK * COPIED)
+        for start, stop in late_chunks:
+            run = raw_late[:, PACK * (start - copied[1]) : PACK * (stop - copied[1])]
+            raw[start] = run.rearrange("p (j c) -> p j c", j=PACK)
             for j in range(PACK):
-                begin = split if start == first[0] and j < PACK - 1 else start
-                nc.scalar.activation(raw[start][:, j, begin - start :], picked_x(j, begin, stop), COPY)
+                fetch_x(start, j, start, stop)
 
         woven = {}
 
@@ -129,17 +138,24 @@ def tile_moe_pre_lin_none_kernel(
             base = max(s for s in woven if s <= start)
             return woven[base][:, PACK * (start - base) : PACK * (stop - base)]
 
-        new_woven(0, OWN, "woven_pool")
-        new_woven(OWN, first[1], "woven_first")
-        new_woven(pool_run[1], SLOTS, "woven_last")
+        def pool_times_gate_and_weave(start, stop):
+            nc.gpsimd.tensor_tensor(
+                woven_run(start, stop).rearrange("p (c j) -> p c j", j=PACK),
+                raw[start][:, :, : stop - start].rearrange("p j c -> p c j"),
+                gate_pool[start, stop][:].unsqueeze(2).to_broadcast([P, stop - start, PACK]),
+                MULT,
+            )
+
+        new_woven(0, copied[1], "woven_early")
         nc.gpsimd.tensor_scalar(
-            woven_run(0, OWN).rearrange("p (c j) -> p c j", j=PACK),
+            woven_run(*own).rearrange("p (c j) -> p c j", j=PACK),
             products[:].rearrange("p j c -> p c j"),
             1.0,
             0.0,
             MULT,
             ADD,
         )
+        pool_times_gate_and_weave(*pool_first)
 
         def times_gate_and_weave(start, stop):
             bank = gate_psum.tile([P, BANK], F32, name="gate_bank")
@@ -165,7 +181,8 @@ def tile_moe_pre_lin_none_kernel(
         def multiply(unit, start, stop, empty, banks=psum, tag="acc"):
             base, codes, scale_rows = unit
             acc = banks.tile([P, BANK], F32, name=tag)
-            for s0, s1 in cut(start, stop, C):
+            edges = [start] + list(range(start // C * C + C, stop, C)) + [stop]
+            for s0, s1 in zip(edges, edges[1:]):
                 nc.tensor.matmul_mx(
                     out=acc[:, s0 - start : s1 - start],
                     lhsT=w_codes[:, s0 // C, :].bitcast(FP8X4),
@@ -182,27 +199,23 @@ def tile_moe_pre_lin_none_kernel(
             for s0, s1 in cut(start, stop, BANK):
                 multiply(unit, s0, s1, nc.scalar.copy)
 
-        for piece in cut(*first, BANK):
+        for piece in reversed(cut(*copied, BANK)):
             times_gate_and_weave(*piece)
-        for unit in cut(*first, 2 * BANK) + [(0, OWN)]:
+        for unit in cut(0, copied[1], 2 * BANK):
             quantise_and_multiply(*unit)
-        new_woven(*pool_run, "woven_pool")
-        nc.gpsimd.tensor_tensor(
-            woven_run(*pool_run).rearrange("p (c j) -> p c j", j=PACK),
-            raw[pool_run[0]][:, :, :POOL_SHARE].rearrange("p j c -> p c j"),
-            gate_pool[:].unsqueeze(2).to_broadcast([P, POOL_SHARE, PACK]),
-            MULT,
-        )
-        late = cut(pool_run[1], SLOTS, BANK)
+        new_woven(*pool_second, "woven_early")
+        pool_times_gate_and_weave(*pool_second)
+        new_woven(pool_second[1], SLOTS, "raw_first")
+        late = [(max(start, pool_second[1]), stop) for start, stop in late_chunks]
         for piece in late:
             times_gate_and_weave(*piece)
-        for unit in late[:-1]:
+        for unit in late[:2]:
             quantise_and_multiply(*unit)
-        pool_unit = quantise(*pool_run)
-        last_unit = quantise(*late[-1])
-        multiply(pool_unit, pool_run[0], pool_run[0] + C, nc.vector.tensor_copy)
-        multiply(pool_unit, pool_run[0] + C, pool_run[1], nc.scalar.copy, gate_psum, "gate_bank")
-        for piece in cut(*late[-1], P):
+        pool_unit = quantise(*pool_second)
+        last_unit = quantise(*late[2])
+        multiply(pool_unit, pool_second[0], pool_second[0] + C, nc.vector.tensor_copy)
+        multiply(pool_unit, pool_second[0] + C, pool_second[1], nc.scalar.copy, gate_psum, "gate_bank")
+        for piece in cut(*late[2], P):
             multiply(last_unit, *piece, nc.vector.tensor_copy, gate_psum, "gate_bank")
 
         def picked(r, tokens):

@@ -25,7 +25,8 @@ ADD = mybir.AluOpType.add
 COPY = mybir.ActivationFunctionType.Copy
 
 OWN = 512
-POOL_FIRST = 896
+FIRST_CHUNK = 896
+POOL_FIRST = 832
 COPIED = 896
 LATE_CHUNKS = [1024, 512, 256]
 POOL_SECOND = 512
@@ -50,10 +51,11 @@ def tile_moe_pre_lin_none_kernel(
     with ExitStack() as ctx:
         keep = ctx.enter_context(tc.tile_pool(name="keep", bufs=1))
         after_blocks = ctx.enter_context(tc.tile_pool(name="after_blocks", bufs=1))
-        gate_psum = ctx.enter_context(tc.psum_pool(name="gate_psum", bufs=3))
+        gate_psum = ctx.enter_context(tc.psum_pool(name="gate_psum", bufs=4))
         psum = ctx.enter_context(tc.psum_pool(name="psum", bufs=3))
 
-        own, pool_first, copied = runs([OWN, POOL_FIRST, COPIED], 0)
+        own, first_chunk, copied = runs([OWN, FIRST_CHUNK, COPIED], 0)
+        pool_first = (OWN, OWN + POOL_FIRST)
         late_chunks = runs(LATE_CHUNKS, copied[1])
         pool_second = (copied[1], copied[1] + POOL_SECOND)
 
@@ -106,7 +108,7 @@ def tile_moe_pre_lin_none_kernel(
             return x_rows[j][:].indirect(slot_list[:, start // PER_COLUMN : stop // PER_COLUMN])
 
         raw = {}
-        raw_first = keep.tile([P, PACK, POOL_FIRST], F32, name="raw_first", tag="raw_first", align_bytes=64)
+        raw_first = keep.tile([P, PACK, FIRST_CHUNK], F32, name="raw_first", tag="raw_first", align_bytes=64)
         raw[pool_first[0]] = raw_first[:]
         nc.vector.tensor_copy(raw_first[:, 0, :HELP], picked_x(0, pool_first[0], pool_first[0] + HELP))
         products = keep.tile([P, PACK, OWN], F32, name="products")
@@ -121,7 +123,7 @@ def tile_moe_pre_lin_none_kernel(
             nc.scalar.activation(raw[base][:, j, start - base : stop - base], picked_x(j, start, stop), COPY)
 
         for j in range(PACK):
-            fetch_x(pool_first[0], j, pool_first[0] + (HELP if j == 0 else 0), pool_first[1])
+            fetch_x(first_chunk[0], j, first_chunk[0] + (HELP if j == 0 else 0), first_chunk[1])
         raw_late = after_blocks.tile([P, PACK * (SLOTS - copied[1])], F32, name="raw_late", offset=4 * PACK * COPIED)
         for start, stop in late_chunks:
             run = raw_late[:, PACK * (start - copied[1]) : PACK * (stop - copied[1])]
@@ -159,12 +161,12 @@ def tile_moe_pre_lin_none_kernel(
 
         def times_gate_and_weave(start, stop):
             bank = gate_psum.tile([P, BANK], F32, name="gate_bank")
-            for c0 in range(0, stop - start, P):
-                block = (start + c0) // P
-                column = gate_columns[:, block : block + 1].to_broadcast([P, P])
-                nc.tensor.transpose(bank[:, c0 : c0 + P], column, identity[:])
+            edge = start // P * P
+            for s0 in range(edge, stop, P):
+                column = gate_columns[:, s0 // P : s0 // P + 1].to_broadcast([P, P])
+                nc.tensor.transpose(bank[:, s0 - edge : s0 - edge + P], column, identity[:])
             base = max(s for s in raw if s <= start)
-            gate_view = bank[:, : stop - start].rearrange("p (c i) -> p c i", i=NEAR)
+            gate_view = bank[:, start - edge : stop - edge].rearrange("p (c i) -> p c i", i=NEAR)
             nc.vector.tensor_tensor(
                 woven_run(start, stop).rearrange("p (c i j) -> p c j i", i=NEAR, j=PACK),
                 raw[base][:, :, start - base : stop - base].rearrange("p j (c i) -> p c j i", i=NEAR),
@@ -199,9 +201,10 @@ def tile_moe_pre_lin_none_kernel(
             for s0, s1 in cut(start, stop, BANK):
                 multiply(unit, s0, s1, nc.scalar.copy)
 
-        for piece in reversed(cut(*copied, BANK)):
+        for piece in reversed([(pool_first[1], first_chunk[1])] + cut(*copied, BANK)):
             times_gate_and_weave(*piece)
-        for unit in cut(0, copied[1], 2 * BANK):
+        early = cut(0, copied[1], 2 * BANK)
+        for unit in early[-1:] + early[:-1]:
             quantise_and_multiply(*unit)
         new_woven(*pool_second, "woven_early")
         pool_times_gate_and_weave(*pool_second)

@@ -26,7 +26,7 @@ COPY = mybir.ActivationFunctionType.Copy
 
 OWN = 512
 FIRST_CHUNK = 896
-POOL_FIRST = 832
+POOL_FIRST = 864
 COPIED = 896
 LATE_CHUNKS = [1024, 512, 256]
 POOL_SECOND = 512
@@ -51,6 +51,7 @@ def tile_moe_pre_lin_none_kernel(
     with ExitStack() as ctx:
         keep = ctx.enter_context(tc.tile_pool(name="keep", bufs=1))
         after_blocks = ctx.enter_context(tc.tile_pool(name="after_blocks", bufs=1))
+        after_early = ctx.enter_context(tc.tile_pool(name="after_early", bufs=1))
         gate_psum = ctx.enter_context(tc.psum_pool(name="gate_psum", bufs=4))
         psum = ctx.enter_context(tc.psum_pool(name="psum", bufs=3))
 
@@ -67,7 +68,8 @@ def tile_moe_pre_lin_none_kernel(
         gate_blocks = after_blocks.tile([P, P], F32, name="gate_blocks", offset=4 * (PACK * COPIED - P // 2))
         gate_columns = keep.tile([P, SLOTS // P], F32, name="gate_columns")
         identity = keep.tile([P, P], F32, name="identity")
-        w_codes = keep.tile([P, E, N * PACK], U8, name="w_codes", align_bytes=64)
+        early_experts = copied[1] // C
+        w_late = keep.tile([P, E - early_experts, N * PACK], U8, name="w_late", align_bytes=64)
         w_scale_rows = keep.tile([P, E, N], U8, name="w_scale_rows", align_bytes=64)
         y = keep.tile([P, SLOTS], F32, name="y")
         warm = keep.tile([P, 2], F32, name="warm")
@@ -94,9 +96,8 @@ def tile_moe_pre_lin_none_kernel(
             nc.sync.dma_start(
                 w_scale_rows[32 * quad : 32 * quad + 4, :, :].bitcast(I32), scales_hbm[4 * quad : 4 * quad + 4]
             )
-        for e0 in range(0, E, E // 2):
-            experts = slice(e0, e0 + E // 2)
-            nc.sync.dma_start(w_codes[:, experts, :].bitcast(I32), words_hbm[:, experts, :])
+        for e0, e1 in cut(early_experts, E, 4):
+            nc.sync.dma_start(w_late[:, e0 - early_experts : e1 - early_experts, :].bitcast(I32), words_hbm[:, e0:e1, :])
         for tile, pos in zip(pos_lists, (pos1, pos2, pos3, pos4)):
             nc.sync.dma_start(tile[:], pos)
 
@@ -133,8 +134,8 @@ def tile_moe_pre_lin_none_kernel(
 
         woven = {}
 
-        def new_woven(start, stop, tag):
-            woven[start] = keep.tile([P, PACK * (stop - start)], BF16, name=f"woven{start}", tag=tag, align_bytes=64)
+        def new_woven(start, stop, pool, **place):
+            woven[start] = pool.tile([P, PACK * (stop - start)], BF16, name=f"woven{start}", align_bytes=64, **place)
 
         def woven_run(start, stop):
             base = max(s for s in woven if s <= start)
@@ -148,7 +149,7 @@ def tile_moe_pre_lin_none_kernel(
                 MULT,
             )
 
-        new_woven(0, copied[1], "woven_early")
+        new_woven(0, copied[1], after_early, offset=0)
         nc.gpsimd.tensor_scalar(
             woven_run(*own).rearrange("p (c j) -> p c j", j=PACK),
             products[:].rearrange("p j c -> p c j"),
@@ -187,7 +188,7 @@ def tile_moe_pre_lin_none_kernel(
             for s0, s1 in zip(edges, edges[1:]):
                 nc.tensor.matmul_mx(
                     out=acc[:, s0 - start : s1 - start],
-                    lhsT=w_codes[:, s0 // C, :].bitcast(FP8X4),
+                    lhsT=w_codes[s0 // C].bitcast(FP8X4),
                     lhsT_scale=w_scale_rows[:, s0 // C, :],
                     rhs=codes[:, s0 - base : s1 - base].bitcast(FP8X4),
                     rhs_scale=scale_rows[:, s0 - base : s1 - base],
@@ -201,14 +202,23 @@ def tile_moe_pre_lin_none_kernel(
             for s0, s1 in cut(start, stop, BANK):
                 multiply(unit, s0, s1, nc.scalar.copy)
 
-        for piece in reversed([(pool_first[1], first_chunk[1])] + cut(*copied, BANK)):
+        bank_edge = copied[0] // P * P + BANK
+        for piece in ((bank_edge, copied[1]), (copied[0], bank_edge), (pool_first[1], first_chunk[1])):
             times_gate_and_weave(*piece)
         early = cut(0, copied[1], 2 * BANK)
-        for unit in early[-1:] + early[:-1]:
-            quantise_and_multiply(*unit)
-        new_woven(*pool_second, "woven_early")
+        early = early[-1:] + early[:-1]
+        early_units = [quantise(*run) for run in early]
+        w_early = after_early.tile(
+            [P, early_experts, N * PACK], U8, name="w_early", align_bytes=64, offset=2 * PACK * POOL_SECOND
+        )
+        nc.sync.dma_start(w_early[:].bitcast(I32), words_hbm[:, :early_experts, :])
+        w_codes = [w_early[:, e, :] for e in range(early_experts)] + [w_late[:, e, :] for e in range(E - early_experts)]
+        for unit, run in zip(early_units, early):
+            for piece in cut(*run, BANK):
+                multiply(unit, *piece, nc.scalar.copy)
+        new_woven(*pool_second, after_early, offset=0)
         pool_times_gate_and_weave(*pool_second)
-        new_woven(pool_second[1], SLOTS, "raw_first")
+        new_woven(pool_second[1], SLOTS, keep, tag="raw_first")
         late = [(max(start, pool_second[1]), stop) for start, stop in late_chunks]
         for piece in late:
             times_gate_and_weave(*piece)

from contextlib import ExitStack

import concourse.mybir as mybir
from concourse.masks import make_identity

K, T, E, C, N = 512, 1024, 16, 256, 128
TOP = 4
SLOTS = E * C
P = 128
PACK = 4
PER_COLUMN = 16
BANK = 512
FLOPS = 2 * K * N * SLOTS
BYTES = 4 * K * T + E * K * N + E * 16 * N + 4 * SLOTS + 2 * P * (SLOTS + TOP * T) // PER_COLUMN + 4 * N * T

F32 = mybir.dt.float32
BF16 = mybir.dt.bfloat16
I32 = mybir.dt.int32
U32 = mybir.dt.uint32
U16 = mybir.dt.uint16
U8 = mybir.dt.uint8
FP8X4 = mybir.dt.float8_e4m3fn_x4
MULT = mybir.AluOpType.mult
ADD = mybir.AluOpType.add
COPY = mybir.ActivationFunctionType.Copy

OWN = 512
FIRST_CHUNK = 896
POOL_FIRST = 864
COPIED = 896
LATE_CHUNKS = [1024, 512, 256]
POOL_SECOND = 512
HELP = 192
WINDOW = T + 32
NEAR = 2


def runs(widths, first):
    edges = [first + sum(widths[:i]) for i in range(len(widths) + 1)]
    return list(zip(edges, edges[1:]))


def cut(start, stop, width):
    return [(s, min(s + width, stop)) for s in range(start, stop, width)]


def tile_moe_pre_lin_none_kernel(
    tc, xT, w_words, w_scales, gate, offs, pos1, pos2, pos3, pos4, out
):
    nc = tc.nc
    with ExitStack() as ctx:
        keep = ctx.enter_context(tc.tile_pool(name="keep", bufs=1))
        after_blocks = ctx.enter_context(tc.tile_pool(name="after_blocks", bufs=1))
        after_early = ctx.enter_context(tc.tile_pool(name="after_early", bufs=1))
        gate_psum = ctx.enter_context(tc.psum_pool(name="gate_psum", bufs=4))
        psum = ctx.enter_context(tc.psum_pool(name="psum", bufs=3))

        own, first_chunk, copied = runs([OWN, FIRST_CHUNK, COPIED], 0)
        pool_first = (OWN, OWN + POOL_FIRST)
        late_chunks = runs(LATE_CHUNKS, copied[1])
        pool_second = (copied[1], copied[1] + POOL_SECOND)

        slot_list = keep.tile([P, SLOTS // PER_COLUMN], U16, name="slot_list")
        pos_lists = [keep.tile([P, T // PER_COLUMN], U16, name=f"pos_list{r}") for r in range(TOP)]
        x_rows = [keep.tile([P, WINDOW], F32, name=f"x_rows{j}") for j in range(PACK)]
        gate_own = keep.tile([P, OWN], F32, name="gate_own")
        gate_pool = {run: keep.tile([P, run[1] - run[0]], F32, name=f"gate{run[0]}") for run in (pool_first, pool_second)}
        gate_blocks = after_blocks.tile([P, P], F32, name="gate_blocks", offset=4 * (PACK * COPIED - P // 2))
        gate_columns = keep.tile([P, SLOTS // P], F32, name="gate_columns")
        identity = keep.tile([P, P], F32, name="identity")
        early_experts = copied[1] // C
        w_late = keep.tile([P, E - early_experts, N * PACK], U8, name="w_late", align_bytes=64)
        w_scale_rows = keep.tile([P, E, N], U8, name="w_scale_rows", align_bytes=64)
        y = keep.tile([P, SLOTS], F32, name="y")
        warm = keep.tile([P, 2], F32, name="warm")
        nc.gpsimd.memset(warm[:, 0:1], 0.0)
        nc.scalar.activation(warm[:, 1:2], warm[:, 0:1], COPY)
        make_identity(nc, identity[:])

        x_by_row = xT.rearrange("(p j) t -> j p t", j=PACK)
        gate_rows = gate.rearrange("(p j) s -> j p s", j=PACK)[0]
        blocks_hbm = gate.rearrange("k (b c) -> (k b) c", c=P)[:P, :]
        words_hbm = w_words.rearrange("e a p n r -> p (e a) (n r)").bitcast(I32)
        scales_hbm = w_scales.rearrange("e a q n -> q (e a) n").bitcast(I32)

        nc.gpsimd.memset(w_scale_rows[:].bitcast(I32), 0)
        nc.sync.dma_start(slot_list[:], offs)
        nc.sync.dma_start(x_rows[0][:, :T], x_by_row[0])
        nc.sync.dma_start(gate_own[:], gate_rows[:, :OWN])
        for j in range(1, PACK):
            nc.sync.dma_start(x_rows[j][:, :T], x_by_row[j])
        nc.sync.dma_start(gate_blocks[:], blocks_hbm)
        for run, tile in gate_pool.items():
            nc.sync.dma_start(tile[:], gate_rows[:, run[0] : run[1]])
        for quad in range(4):
            nc.sync.dma_start(
                w_scale_rows[32 * quad : 32 * quad + 4, :, :].bitcast(I32), scales_hbm[4 * quad : 4 * quad + 4]
            )
        for e0, e1 in cut(early_experts, E, 4):
            nc.sync.dma_start(w_late[:, e0 - early_experts : e1 - early_experts, :].bitcast(I32), words_hbm[:, e0:e1, :])
        for tile, pos in zip(pos_lists, (pos1, pos2, pos3, pos4)):
            nc.sync.dma_start(tile[:], pos)

        turned_gate = gate_psum.tile([P, BANK], F32, name="gate_bank")
        nc.tensor.transpose(turned_gate[:, :P], gate_blocks[:], identity[:])
        nc.scalar.copy(out=gate_columns[:], in_=turned_gate[:, : SLOTS // P])

        def picked_x(j, start, stop):
            return x_rows[j][:].indirect(slot_list[:, start // PER_COLUMN : stop // PER_COLUMN])

        raw = {}
        raw_first = keep.tile([P, PACK, FIRST_CHUNK], F32, name="raw_first", tag="raw_first", align_bytes=64)
        raw[pool_first[0]] = raw_first[:]
        nc.vector.tensor_copy(raw_first[:, 0, :HELP], picked_x(0, pool_first[0], pool_first[0] + HELP))
        products = keep.tile([P, PACK, OWN], F32, name="products")
        for j in range(PACK):
            nc.vector.tensor_tensor(products[:, j, :], picked_x(j, *own), gate_own[:], MULT)
        raw_copied = after_blocks.tile([P, PACK, COPIED], F32, name="raw_copied", offset=0)
        raw[copied[0]] = raw_copied[:]
        for j in range(PACK):
            nc.vector.tensor_copy(raw_copied[:, j, :], picked_x(j, *copied))

        def fetch_x(base, j, start, stop):
            nc.scalar.activation(raw[base][:, j, start - base : stop - base], picked_x(j, start, stop), COPY)

        for j in range(PACK):
            fetch_x(first_chunk[0], j, first_chunk[0] + (HELP if j == 0 else 0), first_chunk[1])
        raw_late = after_blocks.tile([P, PACK * (SLOTS - copied[1])], F32, name="raw_late", offset=4 * PACK * COPIED)
        for start, stop in late_chunks:
            run = raw_late[:, PACK * (start - copied[1]) : PACK * (stop - copied[1])]
            raw[start] = run.rearrange("p (j c) -> p j c", j=PACK)
            for j in range(PACK):
                fetch_x(start, j, start, stop)

        woven = {}

        def new_woven(start, stop, pool, **place):
            woven[start] = pool.tile([P, PACK * (stop - start)], BF16, name=f"woven{start}", align_bytes=64, **place)

        def woven_run(start, stop):
            base = max(s for s in woven if s <= start)
            return woven[base][:, PACK * (start - base) : PACK * (stop - base)]

        def pool_times_gate_and_weave(start, stop):
            nc.gpsimd.tensor_tensor(
                woven_run(start, stop).rearrange("p (c j) -> p c j", j=PACK),
                raw[start][:, :, : stop - start].rearrange("p j c -> p c j"),
                gate_pool[start, stop][:].unsqueeze(2).to_broadcast([P, stop - start, PACK]),
                MULT,
            )

        new_woven(0, copied[1], after_early, offset=0)
        nc.gpsimd.tensor_scalar(
            woven_run(*own).rearrange("p (c j) -> p c j", j=PACK),
            products[:].rearrange("p j c -> p c j"),
            1.0,
            0.0,
            MULT,
            ADD,
        )
        pool_times_gate_and_weave(*pool_first)

        def times_gate_and_weave(start, stop):
            bank = gate_psum.tile([P, BANK], F32, name="gate_bank")
            edge = start // P * P
            for s0 in range(edge, stop, P):
                column = gate_columns[:, s0 // P : s0 // P + 1].to_broadcast([P, P])
                nc.tensor.transpose(bank[:, s0 - edge : s0 - edge + P], column, identity[:])
            base = max(s for s in raw if s <= start)
            gate_view = bank[:, start - edge : stop - edge].rearrange("p (c i) -> p c i", i=NEAR)
            nc.vector.tensor_tensor(
                woven_run(start, stop).rearrange("p (c i j) -> p c j i", i=NEAR, j=PACK),
                raw[base][:, :, start - base : stop - base].rearrange("p j (c i) -> p c j i", i=NEAR),
                gate_view.unsqueeze(2).to_broadcast([P, (stop - start) // NEAR, PACK, NEAR]),
                MULT,
            )

        def quantise(start, stop):
            codes = keep.tile([P, stop - start], U32, name=f"codes{start}", align_bytes=64)
            scale_rows = keep.tile([P, stop - start], U8, name=f"scale_rows{start}", align_bytes=64)
            nc.vector.quantize_mx(out=codes[:].bitcast(FP8X4), scales=scale_rows[:], in_=woven_run(start, stop))
            return start, codes, scale_rows

        def multiply(unit, start, stop, empty, banks=psum, tag="acc"):
            base, codes, scale_rows = unit
            acc = banks.tile([P, BANK], F32, name=tag)
            edges = [start] + list(range(start // C * C + C, stop, C)) + [stop]
            for s0, s1 in zip(edges, edges[1:]):
                nc.tensor.matmul_mx(
                    out=acc[:, s0 - start : s1 - start],
                    lhsT=w_codes[s0 // C].bitcast(FP8X4),
                    lhsT_scale=w_scale_rows[:, s0 // C, :],
                    rhs=codes[:, s0 - base : s1 - base].bitcast(FP8X4),
                    rhs_scale=scale_rows[:, s0 - base : s1 - base],
                    start=True,
                    stop=True,
                )
            empty(out=y[:, start:stop], in_=acc[:, : stop - start])

        def quantise_and_multiply(start, stop):
            unit = quantise(start, stop)
            for s0, s1 in cut(start, stop, BANK):
                multiply(unit, s0, s1, nc.scalar.copy)

        bank_edge = copied[0] // P * P + BANK
        for piece in ((bank_edge, copied[1]), (copied[0], bank_edge), (pool_first[1], first_chunk[1])):
            times_gate_and_weave(*piece)
        early = cut(0, copied[1], 2 * BANK)
        early = early[-1:] + early[:-1]
        early_units = [quantise(*run) for run in early]
        w_early = after_early.tile(
            [P, early_experts, N * PACK], U8, name="w_early", align_bytes=64, offset=2 * PACK * POOL_SECOND
        )
        nc.sync.dma_start(w_early[:].bitcast(I32), words_hbm[:, :early_experts, :])
        w_codes = [w_early[:, e, :] for e in range(early_experts)] + [w_late[:, e, :] for e in range(E - early_experts)]
        for unit, run in zip(early_units, early):
            for piece in cut(*run, BANK):
                multiply(unit, *piece, nc.scalar.copy)
        new_woven(*pool_second, after_early, offset=0)
        pool_times_gate_and_weave(*pool_second)
        new_woven(pool_second[1], SLOTS, keep, tag="raw_first")
        late = [(max(start, pool_second[1]), stop) for start, stop in late_chunks]
        for piece in late:
            times_gate_and_weave(*piece)
        for unit in late[:2]:
            quantise_and_multiply(*unit)
        pool_unit = quantise(*pool_second)
        last_unit = quantise(*late[2])
        multiply(pool_unit, pool_second[0], pool_second[0] + C, nc.vector.tensor_copy)
        multiply(pool_unit, pool_second[0] + C, pool_second[1], nc.scalar.copy, gate_psum, "gate_bank")
        for piece in cut(*late[2], P):
            multiply(last_unit, *piece, nc.vector.tensor_copy, gate_psum, "gate_bank")

        def picked(r, tokens):
            return y[:].indirect(pos_lists[r][:, tokens.start // PER_COLUMN : tokens.stop // PER_COLUMN])

        fetched = [keep.tile([P, T], F32, name=f"fetched{r}") for r in range(3)]
        totals = [keep.tile([P, T], F32, name=f"total{r}") for r in range(TOP)]
        lead, mid, late, last = slice(0, 256), slice(256, 512), slice(512, 768), slice(768, T)
        both = slice(0, 512)

        def fetch(r, tokens):
            nc.scalar.activation(fetched[r][:, tokens], picked(r, tokens), COPY)

        def add_picked(to, r, tokens, onto):
            nc.vector.tensor_tensor(totals[to][:, tokens], picked(r, tokens), onto[:, tokens], ADD)

        def add_fetched(to, r, tokens):
            nc.vector.tensor_tensor(totals[to][:, tokens], totals[to - 1][:, tokens], fetched[r][:, tokens], ADD)

        for r, tokens in ((0, mid), (0, slice(512, T)), (0, lead), (1, both), (1, slice(512, T)), (2, last)):
            fetch(r, tokens)
        nc.vector.tensor_copy(totals[0][:, lead], picked(2, lead))
        add_picked(1, 2, mid, fetched[0])
        add_picked(1, 3, lead, totals[0])
        add_picked(0, 2, late, fetched[0])
        add_picked(2, 3, mid, totals[1])
        add_fetched(2, 0, lead)
        add_picked(1, 3, last, fetched[0])
        add_fetched(3, 1, both)
        nc.sync.dma_start(out[:, both], totals[3][:, both])
        add_picked(2, 3, late, totals[0])
        add_fetched(2, 1, last)
        add_fetched(3, 1, late)
        nc.scalar.dma_start(out[:, late], totals[3][:, late])
        add_fetched(3, 2, last)
        nc.sync.dma_start(out[:, last], totals[3][:, last])
